import numpy as np, ml_dtypes
CORES = [35,38,43,46]
N = 4
import mx_ref
BF = ml_dtypes.bfloat16
def entries(a):
    return np.ascontiguousarray(a.T).reshape(-1)
def table(e):
    return np.ascontiguousarray(np.reshape(e, (-1, 16)).T).astype(np.int32)
def cols(t, e):
    v = np.concatenate([t.reshape(128, -1, 4), np.zeros((128, 1, 4), BF)], axis=1)
    return np.ascontiguousarray(v[:, e]).reshape(128, -1)
def tile(rs):
    return np.stack(rs, axis=2).reshape(128, -1).astype(BF)
def cut(t, i, w=512):
    return t[:, w * i:w * i + w]
def f(rng, *shape):
    return mx_ref.flush((rng.standard_normal(shape, dtype=np.float32) * np.exp2(rng.integers(-2, 3, shape[:-1] + (1,)))).astype(BF))
def wide(rng, *shape, cols=0):
    v = rng.standard_normal(shape, dtype=np.float32) * np.exp2(rng.integers(-12, 13, shape)).astype(np.float32)
    if cols: v *= np.repeat(np.exp2(rng.integers(-cols, cols + 1, shape[:-2] + (1, shape[-1] // 4))) * (rng.random(shape[:-2] + (1, shape[-1] // 4)) > 0.0625), 4, axis=-1).astype(np.float32)
    return mx_ref.flush(v.astype(BF))
S, C1, C2 = 256, 48, 80
def pack(nb):
    return {"nb0": np.stack([table(e) for e in nb[0].reshape(N, S)]), "nb1": np.stack([table(e) for e in nb[1].reshape(N, S)])}
def lists(rng):
    pool = [[(q * S + rng.permutation(S)[:rng.integers(1, 3 * C1 // 4 + 1)]).tolist() for q in range(N)] for r in range(N)]
    skew = []
    for r in range(N):
        p = np.exp2(rng.integers(0, 4, N)).astype(float); p[r] = 0
        skew.append(np.divide(p, p.sum()))
    who = {n: [] for n in range(N * S)}
    near, hand = {}, {}
    for r in range(N):
        for q in range(N):
            if q == r: continue
            for n in pool[r][q]: who[n].append(r)
            near[r, q] = set(pool[r][q]); hand[r, q] = set(pool[r][q])
    def one(r):
        if rng.random() < 0.6: return int(r * S + rng.integers(0, S))
        p = pool[r][int(rng.choice(N, p=skew[r]))]
        return p[rng.integers(0, len(p))]
    def fits(n, w):
        return all((w // S == r or len(near[r, w // S] | {w}) <= C2) and len(hand[r, n // S] | {w}) <= C2 for r in who[n])
    nb = np.zeros((2, N * S), int)
    for n in rng.permutation(N * S).tolist():
        for k in range(2):
            for _ in range(8):
                w = one(n // S)
                if fits(n, w): break
            else: w = n
            nb[k, n] = w
            for r in who[n]:
                if w // S != r: near[r, w // S].add(w)
                hand[r, n // S].add(w)
    for r in range(N):
        free = rng.permutation([n for n in range(r * S, r * S + S) if not who[n]])
        nb[1, free[:S // 20]] = nb[0, free[:S // 20]]
        for k in range(2):
            p = rng.permutation(free)[:2 * (S >> 6)]
            nb[k, p] = p[::-1]
    return pack(nb)
def weights(rng, n):
    return np.stack([f(rng, 128, 512 * n)] * N)
def setup_inputs(rng):
    return {"x": f(rng, N, 128, 4 * S), "a": weights(rng, 8), "v": weights(rng, 2), "u": weights(rng, 2), **lists(rng)}
def setup_inputs_apart(rng):
    d = setup_inputs(rng)
    nb = np.zeros((2, N * S), int)
    e, m = C2 - C1, S - (N - 1) * C1
    h = min(-(-m // (N - 1)), e - 2)
    p = [q * S + rng.permutation(S) for q in range(N)]
    F, H = {}, {}
    for q in range(N):
        for i in range(N - 1):
            r = (q + 1 + i) % N
            F[r, q] = p[q][C1 * i:C1 * i + C1]
            H[r, q] = p[q][(N - 1) * C1 + (h * i + np.arange(h)) % m]
    for r, q in F:
        s = (q + 1) % N
        if s == r: s = (q + 2) % N
        D = np.concatenate([H[r, q], rng.permutation(F[q, s])[:e - h]])
        k = (r + q) % 2
        nb[k, F[r, q]] = rng.permutation(F[q, r])
        nb[1 - k, F[r, q]] = np.concatenate([rng.permutation(D), F[q, r][:C1 - e]])
    for r in range(N):
        rest = p[r][(N - 1) * C1:]
        far = np.concatenate([F[r, q] for q in range(N) if q != r])
        for k in range(2):
            must = [int(n) for q in range(N) if q != r and (r + q) % 2 != k for n in F[r, q][C1 - e:e]]
            nb[k, rest] = rng.permutation(must + rng.choice(np.concatenate([far, p[r]]), m - len(must)).tolist())
    return {**d, **pack(nb)}
def setup_inputs_full(rng):
    d = setup_inputs(rng)
    nb = np.zeros((2, N * S), int)
    p = [q * S + rng.permutation(S) for q in range(N)]
    B = [e[:C1] for e in p]
    for q in range(N):
        some = rng.permutation(np.concatenate(B))[:C1]
        nb[:, B[q]] = rng.permutation(np.concatenate([p[q][C1:C2], some, rng.choice(some, 2 * C1 - C2)])).reshape(2, C1)
        rest = p[q][C1:]
        far = np.concatenate([B[s] for s in range(N) if s != q])
        for k in range(2):
            nb[k, rest] = rng.permutation(np.concatenate([far, rng.choice(np.concatenate([far, p[q]]), len(rest) - len(far))]))
    return {**d, **pack(nb)}
def setup_inputs_hub(rng):
    d = setup_inputs(rng)
    nb = np.zeros((2, N * S), int)
    for r in range(N):
        for k in range(2): nb[k, r * S:r * S + S] = (r + rng.integers(1, N)) % N * S + rng.integers(0, S)
    return {**d, **pack(nb)}
def setup_inputs_spread(rng):
    d = setup_inputs(rng); d["x"] = wide(rng, N, 128, 4 * S); return d
def setup_inputs_most(rng):
    d = setup_inputs(rng)
    nb = np.zeros((2, N * S), int)
    p = [q * S + rng.permutation(S) for q in range(N)]
    B = [e[:C1] for e in p]
    for q in range(N):
        nb[:, B[q]] = rng.permutation(np.concatenate([p[q][:C2], rng.choice(p[q][:C2], 2 * C1 - C2)])).reshape(2, C1)
        far = np.concatenate([B[s] for s in range(N) if s != q])
        must = np.concatenate([far, p[q][C2:]])
        nb[:, p[q][C1:]] = rng.permutation(np.concatenate([must, rng.choice(np.concatenate([far, p[q]]), 2 * (S - C1) - len(must))])).reshape(2, S - C1)
    return {**d, **pack(nb)}
def check_inputs(d):
    b = []
    nb = np.stack([np.concatenate([entries(e) for e in d[n]]) for n in ("nb0", "nb1")])
    for n in ("a", "v", "u"):
        if (d[n] != d[n][:1]).any(): b.append(n + " isn't the same on all ranks")
    if nb.min() < 0 or nb.max() >= N * S: return b + ["nb0, nb1"]
    for r in range(N):
        own = nb[:, r * S:r * S + S]
        first = np.unique(own)
        near = np.unique(np.concatenate([first, nb[0][first], nb[1][first]]))
        for q in range(N):
            if q == r: continue
            if (first // S == q).sum() > C1: b.append("too many neighbours on one other rank")
            if (near // S == q).sum() > C2: b.append("too many nodes of one other rank in two steps")
            behind = np.concatenate([nb[k][own[k][own[k] // S == q]] for k in range(2)])
            if len(np.unique(behind)) > C2: b.append("too many nodes behind neighbours on one other rank")
    return b
def product(w, t, e):
    n, i = np.unique(e, return_inverse=True)
    n = np.concatenate([n, np.full(-len(n) % 16, n[0])])
    return mx_ref.matmul(mx_ref.quantize(np.ascontiguousarray(w)), mx_ref.quantize(cols(t, n)))[:, i.reshape(-1)]
def reference(x, a, v, u, nb0, nb1):
    nb = np.stack([np.concatenate([entries(e) for e in n]) for n in (nb0, nb1)])
    x = np.concatenate(list(x), axis=1)
    named = np.unique(nb)
    R = []
    for b in range(4):
        P = product(cut(a[0], b), x, nb[0][named]) + product(cut(a[0], 4 + b), x, nb[1][named])
        R.append(np.maximum(P, np.float32(0)) * np.float32(0.05))
    h = np.zeros((128, N * S, 4), BF)
    h[:, named] = tile(R).reshape(128, -1, 4)
    h = h.reshape(128, -1)
    y = product(cut(v[0], 0), h, nb[0]) + product(cut(v[0], 1), h, nb[1]) + product(cut(u[0], 0), x, nb[0][nb[0]]) + product(cut(u[0], 1), x, nb[1][nb[1]])
    return {"y": np.stack([y[:, r * S:r * S + S] for r in range(N)])}

@@ -1,0 +1,420 @@
+import numpy as np
+from concourse.bass import DstId, RemoteDMATransfer
+from concourse.mybir import dt, AluOpType, AxisListType, ActivationFunctionType
+
+S = 256
+C1 = 48
+RC = 3 * C1
+XT = S + RC
+CODE = "float8_e4m3fn_x4"
+
+SCRATCH = {
+    "nbi": ("sbuf", [128, 32], "int32"),
+    "w": ("sbuf", [128, 32], "uint16"),
+    "band": ("sbuf", [128, 1120], "bfloat16"),
+    "jd": ("sbuf", [128, 32], "float32"),
+    "li": ("sbuf", [128, 8], "int32"),
+    "lu": ("sbuf", [128, 8], "uint16"),
+    "ti": ("sbuf", [128, 2], "int32"),
+    "tq": ("sbuf", [128, 2], "int32"),
+    "thr": ("sbuf", [128, 4], "float32"),
+    "mi": ("sbuf", [128, 512], "int32"),
+    "mj": ("sbuf", [128, 512], "int32"),
+    "mask": ("sbuf", [128, 512], "float32"),
+    "rli": ("sbuf", [128, 18], "int32"),
+    "rl": ("sbuf", [128, 18], "uint16"),
+    "junk": ("sbuf", [128, 2048], "bfloat16"),
+    "cnt": ("sbuf", [128, 8], "float32"),
+    "cint": ("sbuf", [128, 8], "int32"),
+    "clo": ("sbuf", [128, 8], "int32"),
+    "fx": ("sbuf", [128, 256], "bfloat16"),
+    "fy": ("sbuf", [128, 256], "bfloat16"),
+    "dd": ("sbuf", [128, 256], "bfloat16"),
+    "jf": ("sbuf", [128, 512], "bfloat16"),
+    "jv": ("sbuf", [128, 256], "bfloat16"),
+    "ss": ("sbuf", [128, 4], "float32"),
+    "fu": ("sbuf", [128, 3], "uint16"),
+    "rf": ("sbuf", [128, 16], "uint16"),
+    "pm": ("sbuf", [128, 1024], "float32"),
+    "pf": ("sbuf", [128, 512], "float32"),
+    "m1": ("sbuf", [128, 512], "float32"),
+    "sb1": ("sbuf", [128, 528], "float32"),
+    "m2": ("sbuf", [128, 288], "float32"),
+    "sb2": ("sbuf", [128, 304], "float32"),
+    "cpi": ("sbuf", [128, 18], "int32"),
+    "cp": ("sbuf", [128, 18], "uint16"),
+    "pi": ("sbuf", [128, 32], "int32"),
+    "pu": ("sbuf", [128, 32], "uint16"),
+    "pt": ("sbuf", [128, 32], "int32"),
+    "pg": ("sbuf", [128, 32], "int32"),
+    "ptg": ("sbuf", [128, 32], "int32"),
+    "pq": ("sbuf", [128, 32], "int32"),
+    "pk": ("sbuf", [128, 16], "int32"),
+    "pr": ("sbuf", [128, 32], "int32"),
+    "p2": ("sbuf", [128, 32], "uint16"),
+    "xt": ("sbuf", [128, 1024], "bfloat16"),
+    "at": ("sbuf", [128, 4096], "bfloat16"),
+    "vt": ("sbuf", [128, 1024], "bfloat16"),
+    "ut": ("sbuf", [128, 1024], "bfloat16"),
+    "ho": ("sbuf", [128, 1024], "bfloat16"),
+    "hr": ("sbuf", [128, 4 * RC], "bfloat16"),
+    "yb": ("sbuf", [128, 256], "float32"),
+}
+for _n, _w in (("ca", 1024), ("cv", 256), ("cu", 256),
+               ("x0", S),
+               ("s1", RC),
+               ("xb", XT),
+               ("s2", 2 * RC),
+               ("w2", 2 * S + 2 * RC),
+               ("xr", 2 * RC),
+               ("xx", 2 * S),
+               ("hb", XT),
+               ("hg", 2 * S)):
+    SCRATCH[_n + "_c"] = ("sbuf", [128, _w], CODE)
+    SCRATCH[_n + "_s"] = ("sbuf", [128, _w], "uint8")
+for _i in range(8):
+    SCRATCH["ps%d" % _i] = ("psum", [128, 512], "float32")
+
+SEMAPHORES = ["sv", "sa", "st", "sp",
+              "ln", "lx", "la0", "la1", "lu_", "lv_",
+              "rq", "xc", "xs", "bc", "bs", "ls",
+              "y0", "y1"]
+
+
+def rank_program(g, core, T, topo):
+    rank = T.rank_of(core)
+    if rank is None:
+        return
+    A = AluOpType
+    F = ActivationFunctionType
+    V, ACT, TE, SY = g.vector, g.scalar, g.tensor, g.sync
+    sem = T.sem
+    cores = list(T.cores)
+    n = len(cores)
+    count = {"sv": 0, "sa": 0, "st": 0, "sp": 0}
+    seen = {}
+
+    def done(name, ins):
+        ins.then_inc(sem[name], 1)
+        count[name] += 1
+        return (name, count[name])
+
+    def v(ins):
+        return done("sv", ins)
+
+    def a(ins):
+        return done("sa", ins)
+
+    def t(ins):
+        return done("st", ins)
+
+    def p(ins):
+        return done("sp", ins)
+
+    def need(eng, tag, *marks):
+        best = {}
+        for name, c in marks:
+            best[name] = max(best.get(name, 0), c)
+        for name, c in best.items():
+            if seen.get((tag, name), 0) < c:
+                eng.wait_ge(sem[name], c)
+                seen[tag, name] = c
+
+    def others(r):
+        return [q for q in range(n) if q != r]
+
+    def lanes(r):
+        me = cores[r]
+        off = [q for q in others(r) if topo.chip(cores[q]) != topo.chip(me)]
+        on = [q for q in others(r) if topo.chip(cores[q]) == topo.chip(me)]
+        res, used = {}, []
+        for i, q in enumerate(off):
+            e = topo.engines(me, cores[q])
+            k = len(e) // len(off)
+            res[q] = e[i * k:(i + 1) * k]
+            used += res[q]
+        for i, q in enumerate(on):
+            e = [x for x in topo.engines(me, cores[q]) if x not in used]
+            res[q] = e[i::2 * len(on)]
+        return res
+
+    lane = lanes(rank)
+    into = sum(len(lanes(q)[rank]) for q in others(rank))
+    sent = [0]
+
+    def send(pieces, rsem):
+        tr = []
+        for q, (src, dst) in pieces.items():
+            rid, pid, _ = topo.addr(cores[q])
+            m = 0
+            for e in lane[q]:
+                m |= 1 << e
+            tr.append(RemoteDMATransfer(dst_ids=[DstId(rid=rid, pnc=pid)], dma_engine_mask=m, remote_sem=sem[rsem],
+                                        src=src, dst=dst, alu_op=0))
+            sent[0] += len(lane[q])
+        g.remote_dma_fused(tr, local_sem=sem["ls"])
+
+    def codes(name, lo, hi):
+        return T[name + "_c"][:, lo:hi].bitcast(dt.uint8)
+
+    def pick_c(out, lo, hi, win, wlo, whi, off):
+        return v(V.tensor_copy(T[out + "_c"][:, lo:hi].bitcast(dt.uint32),
+                               T[win + "_c"][:, wlo:whi].bitcast(dt.uint32).indirect(off)))
+
+    def pick_s(out, lo, hi, win, wlo, whi, off):
+        return a(ACT.activation(T[out + "_s"][:, lo:hi], T[win + "_s"][:, wlo:whi].indirect(off), F.Copy))
+
+    def quad(q):
+        return 32 * q, 32 * q + 32
+
+    SY.dma_start(T.nbi[0:16, 0:16], T.nb0[:]).then_inc(sem["ln"], 16)
+    ACT.dma_start(T.nbi[0:16, 16:32], T.nb1[:]).then_inc(sem["ln"], 16)
+    SY.dma_start(T.nbi[16:32, 0:16], T.nb0[:]).then_inc(sem["ln"], 16)
+    ACT.dma_start(T.nbi[16:32, 16:32], T.nb1[:]).then_inc(sem["ln"], 16)
+    SY.dma_start(T.xt[:], T.x[:]).then_inc(sem["lx"], 16)
+    SY.dma_start(T.at[:, 0:2048], T.a[:, 0:2048]).then_inc(sem["la0"], 16)
+    SY.dma_start(T.at[:, 2048:4096], T.a[:, 2048:4096]).then_inc(sem["la1"], 16)
+    SY.dma_start(T.ut[:], T.u[:]).then_inc(sem["lu_"], 16)
+    SY.dma_start(T.vt[:], T.v[:]).then_inc(sem["lv_"], 16)
+
+    k_jd = p(g.iota(T.jd[:], [[1, 32]], 0, -1, allow_small_or_imprecise_dtypes=True))
+    k_li = p(g.iota(T.li[:], [[1, 4], [0, 2]], 0, 0))
+    k_ti = p(g.iota(T.ti[:], [[0, 2]], 0, 1))
+    k_mi = p(g.iota(T.mi[:], [[0, 32], [1, 16]], 128, -1))
+    k_rl = p(g.iota(T.rli[:], [[16, 2], [32, 9]], 0, 0))
+    k_po = p(g.iota(T.pm[:, S * rank:S * rank + S], [[1, S]], 0, 0, allow_small_or_imprecise_dtypes=True))
+
+    k = v(V.memset(T.band[:], 0.0))
+    need(V, "v", k, k_jd)
+    for q in range(n):
+        lo, hi = quad(q)
+        c = 96 + S * q
+        v(V.tensor_scalar(T.band[lo:hi, c:c + 32], T.jd[lo:hi, :], float(-lo), None, A.is_equal))
+        k_band = v(V.tensor_scalar(T.band[lo:hi, c + 128:c + 160], T.jd[lo:hi, :], float(-lo), 1024.0, A.is_equal, A.mult))
+    need(V, "v", k_ti)
+    k_l = v(V.tensor_copy(T.lu[:], T.li[:]))
+    k = v(V.tensor_scalar(T.tq[:], T.ti[:], 15, None, A.bitwise_and))
+    v(V.memset(T.jv[:, 240:256], -255.0))
+    v(V.memset(T.sb1[:, 0:16], 0.0))
+    v(V.memset(T.sb2[:, 0:16], 0.0))
+    need(V, "v", k)
+    for c in range(3):
+        k_thr = v(V.tensor_scalar(T.thr[:, c:c + 1], T.tq[:, 0:1], 16 * c + 0.5, None, A.add))
+
+    V.wait_ge(sem["ln"], 64)
+    for q in range(n):
+        lo, hi = quad(q)
+        k_w = v(V.tensor_copy(T.w[lo:hi, :], T.nbi[0:32, :]))
+    need(ACT, "a", k_w)
+    for i in range(3):
+        k_ca = a(ACT.activation(T.junk[:, 512 * i:512 * i + 512], T.band[:, 96 - 32 * i:1120 - 32 * i].indirect(T.w[:, 0:32]),
+                                F.Copy, accum_out=T.cnt[:, i:i + 1]))
+    need(V, "v", k_w)
+    k = v(V.tensor_copy(T.junk[:, 1536:2048], T.band[:, 0:1024].indirect(T.w[:, 0:32])))
+    need(V, "v", k)
+    k_cv = v(V.tensor_reduce(T.cnt[:, 3:4], T.junk[:, 1536:2048], AxisListType.X, A.add))
+    need(V, "v", k_cv, k_ca, k_l)
+    k = v(V.tensor_copy(T.cint[:, 0:4], T.cnt[:, 0:4]))
+    k_h = v(V.tensor_scalar(T.fx[:, 128:256], T.cnt[:, 0:4].indirect(T.lu[:, 0:8]), 1023.5, None, A.is_ge))
+    need(V, "v", k)
+    k = v(V.tensor_scalar(T.clo[:, 0:4], T.cint[:, 0:4], 1023, None, A.bitwise_and))
+    need(V, "v", k)
+    k = v(V.tensor_scalar(T.fx[:, 0:128], T.clo[:, 0:4].indirect(T.lu[:, 0:8]), 0.5, None, A.is_ge))
+    need(V, "v", k, k_h)
+    k = v(V.transpose(T.fy[:], T.fx[:]))
+    need(V, "v", k)
+    k_d = v(V.tensor_tensor_scan(T.dd[:], T.fy[:], T.fy[:], 0.0, A.add, A.max))
+    need(ACT, "a", k_d)
+    for c in range(2):
+        k_sa = a(ACT.activation(T.jf[:, 256 * c:256 * c + 255], T.dd[:, 0:255], F.Sign, bias=T.thr[:, c:c + 1], scale=-1.0,
+                                accum_out=T.ss[:, c:c + 1]))
+    need(V, "v", k_d)
+    k = v(V.tensor_scalar(T.jv[:, 0:255], T.dd[:, 0:255], T.thr[:, 2:3], 2.0, A.is_le, A.mult))
+    need(V, "v", k)
+    k = v(V.tensor_reduce(T.ss[:, 2:3], T.jv[:], AxisListType.X, A.add))
+    need(V, "v", k, k_sa)
+    k_fu = v(V.tensor_scalar(T.fu[:], T.ss[:, 0:3], 255.0, 0.5, A.add, A.mult))
+
+    need(g, "g", k_fu)
+    send({q: (T.fu[:], T.rf[:, 3 * others(q).index(rank):3 * others(q).index(rank) + 3]) for q in others(rank)}, "rq")
+
+    V.wait_ge(sem["lx"], 16)
+    k_x0 = v(V.quantize_mx(T.x0_c[:], T.x0_s[:], T.xt[:]))
+    k_xb = v(V.quantize_mx(T.xb_c[:, 0:S], T.xb_s[:, 0:S], T.xt[:]))
+    turn = 0
+    k_pm = []
+    for i, q in enumerate(others(rank)):
+        ql, qh = quad(q)
+        base = float(S - 1 + C1 * i)
+        for z in range(n):
+            lo, hi = quad(z)
+            out = T.pm[lo:hi, S * q:S * q + S]
+            if turn % 3 == 0:
+                k_pm.append(v(V.tensor_scalar(out, T.dd[ql:qh, :], base, None, A.add)))
+            else:
+                k_pm.append(a(ACT.activation(out, T.dd[ql:qh, :], F.Copy, bias=base)))
+            turn += 1
+    need(V, "v", k_mi)
+    k = v(V.tensor_scalar(T.mj[:], T.mi[:], 15, None, A.bitwise_and))
+    need(V, "v", k)
+    k_mask = v(V.tensor_scalar(T.mask[:], T.mj[:], 0.0, None, A.is_equal))
+    V.wait_ge(sem["la0"], 16)
+    k_a0 = v(V.quantize_mx(T.ca_c[:, 0:512], T.ca_s[:, 0:512], T.at[:, 0:2048]))
+
+    V.wait_ge(sem["rq"], into)
+    sl, sh = quad(rank)
+    for z in range(n):
+        if z != rank:
+            lo, hi = quad(z)
+            k_rf = v(V.tensor_copy(T.rf[lo:hi, 0:9], T.rf[sl:sh, 0:9]))
+    need(V, "v", k_rf, k_x0)
+    k_c = pick_c("s1", 0, RC, "x0", 0, S, T.rf[:, 0:9])
+    need(ACT, "a", k_rf, k_x0)
+    k_s = pick_s("s1", 0, RC, "x0", 0, S, T.rf[:, 0:9])
+
+    def at(q, size):
+        i, j = others(rank).index(q), others(q).index(rank)
+        return size * i, size * j
+
+    need(g, "g", k_c)
+    send({q: (codes("s1", at(q, C1)[0], at(q, C1)[0] + C1), codes("xb", S + at(q, C1)[1], S + at(q, C1)[1] + C1))
+          for q in others(rank)}, "xc")
+    need(g, "g", k_s)
+    send({q: (T.s1_s[:, at(q, C1)[0]:at(q, C1)[0] + C1], T.xb_s[:, S + at(q, C1)[1]:S + at(q, C1)[1] + C1])
+          for q in others(rank)}, "xs")
+
+    need(ACT, "a", k_po, *k_pm)
+    k_pf = a(ACT.activation(T.pf[:], T.pm[:].indirect(T.w[:, 0:32]), F.Copy))
+    need(V, "v", k_mask, k_po, *k_pm)
+    k_m1 = v(V.tensor_tensor(T.m1[:], T.pm[:].indirect(T.w[:, 0:32]), T.mask[:], A.mult))
+    need(V, "v", k_pf)
+    for i in range(2):
+        k = v(V.tensor_tensor(T.m2[:, RC * i:RC * i + RC], T.pf[:, S * i:S * i + S].indirect(T.rf[:, 0:9]), T.mask[:, 0:RC],
+                              A.mult))
+    need(V, "v", k)
+    k = v(V.tensor_tensor_scan(T.sb2[:, 16:304], T.m2[:], T.m2[:], 0.0, A.add, A.max))
+    k_sb1 = v(V.tensor_tensor_scan(T.sb1[:, 16:528], T.m1[:], T.m1[:], 0.0, A.add, A.max))
+    need(V, "v", k)
+    for i in range(2):
+        e = 15 + RC * i
+        k = v(V.tensor_tensor(T.cpi[:, i:18:2], T.sb2[:, e + 16:e + 16 + 129:16], T.sb2[:, e:e + 129:16], A.subtract))
+    need(V, "v", k)
+    k_cp = v(V.tensor_copy(T.cp[:], T.cpi[:]))
+    k_pi = v(V.tensor_tensor(T.pi[:], T.sb1[:, 31:528:16], T.sb1[:, 15:512:16], A.subtract))
+    need(V, "v", k_pi)
+    k_pu = v(V.tensor_copy(T.pu[:], T.pi[:]))
+    V.wait_ge(sem["la1"], 16)
+    k_a1 = v(V.quantize_mx(T.ca_c[:, 512:1024], T.ca_s[:, 512:1024], T.at[:, 2048:4096]))
+
+    V.wait_ge(sem["xc"], into)
+    need(V, "v", k_cp, k_pu, k_xb)
+    k_c = pick_c("s2", 0, 2 * RC, "xb", 0, XT, T.cp[:, 0:18])
+    ACT.wait_ge(sem["xs"], into)
+    need(ACT, "a", k_cp, k_pu, k_xb)
+    k_s = pick_s("s2", 0, 2 * RC, "xb", 0, XT, T.cp[:, 0:18])
+    W = 2 * C1
+    need(g, "g", k_c)
+    send({q: (codes("s2", at(q, W)[0], at(q, W)[0] + W), codes("w2", 2 * S + at(q, W)[1], 2 * S + at(q, W)[1] + W))
+          for q in others(rank)}, "bc")
+    need(g, "g", k_s)
+    send({q: (T.s2_s[:, at(q, W)[0]:at(q, W)[0] + W], T.w2_s[:, 2 * S + at(q, W)[1]:2 * S + at(q, W)[1] + W])
+          for q in others(rank)}, "bs")
+
+    k_c = pick_c("w2", 0, 2 * S, "xb", 0, XT, T.pu[:, 0:32])
+    k_s = pick_s("w2", 0, 2 * S, "xb", 0, XT, T.pu[:, 0:32])
+
+    def mm(out, wt, wcol, mv, c, width, start, stop):
+        return t(TE.matmul_mx(out, T[wt + "_c"][:, wcol:wcol + 128], T[wt + "_s"][:, wcol:wcol + 128],
+                              T[mv + "_c"][:, c:c + width], T[mv + "_s"][:, c:c + width], start, stop))
+
+    def layer(bank, mv, width):
+        ks = []
+        for b in range(4):
+            out = T["ps%d" % (bank + b)][:, 0:width]
+            mm(out, "ca", 128 * b, mv, 0, width, True, False)
+            ks.append(mm(out, "ca", 512 + 128 * b, mv, width, width, False, True))
+        return ks
+
+    def relu(b, bank, width, tile):
+        out = T[tile][:, b:4 * width:4]
+        src = T["ps%d" % (bank + b)][:, 0:width]
+        if b % 2:
+            return v(V.tensor_scalar(out, src, 0.0, 0.05, A.max, A.mult))
+        return a(ACT.activation(out, src, F.Relu, scale=0.05))
+
+    need(TE, "t", k_c, k_s, k_a0, k_a1)
+    ks = layer(0, "w2", S)
+    k_t = v(V.tensor_scalar(T.pt[:], T.pi[:], 1008, None, A.bitwise_and))
+    k_g = v(V.tensor_scalar(T.pg[:], T.pi[:], float(S), None, A.is_ge))
+    need(V, "v", k_t, k_g)
+    k = v(V.tensor_tensor(T.ptg[:], T.pt[:], T.pg[:], A.mult))
+    v(V.tensor_scalar(T.pk[:], T.pg[:, 16:32], float(16 - S), float(S), A.mult, A.add))
+    need(V, "v", k)
+    k = v(V.tensor_tensor(T.pq[:], T.pi[:], T.ptg[:], A.add))
+    need(V, "v", k)
+    k_p2 = v(V.tensor_copy(T.p2[:, 0:16], T.pq[:, 0:16]))
+    k = v(V.tensor_tensor(T.pr[:, 16:32], T.pq[:, 16:32], T.pk[:], A.add))
+    need(V, "v", k, k_rl)
+    k_p2 = v(V.tensor_copy(T.p2[:, 16:32], T.pr[:, 16:32]))
+    k_rlu = v(V.tensor_scalar(T.rl[:], T.rli[:], T.thr[:, 0:1], -0.5, A.add, A.add))
+    V.wait_ge(sem["lu_"], 16)
+    k_u = v(V.quantize_mx(T.cu_c[:], T.cu_s[:], T.ut[:]))
+    V.wait_ge(sem["lv_"], 16)
+    k_v = v(V.quantize_mx(T.cv_c[:], T.cv_s[:], T.vt[:]))
+    kr = []
+    for b in range(4):
+        need(*((V, "v") if b % 2 else (ACT, "a")), ks[b])
+        kr.append(relu(b, 0, S, "ho"))
+    need(V, "v", *kr)
+    k_ho = v(V.quantize_mx(T.hb_c[:, 0:S], T.hb_s[:, 0:S], T.ho[:]))
+
+    V.wait_ge(sem["bc"], into)
+    need(V, "v", k_rlu, k_p2)
+    kc = pick_c("xr", 0, 2 * RC, "w2", 2 * S, 2 * S + 2 * RC, T.rl[:, 0:18])
+    ACT.wait_ge(sem["bs"], into)
+    need(ACT, "a", k_rlu, k_p2)
+    ksc = pick_s("xr", 0, 2 * RC, "w2", 2 * S, 2 * S + 2 * RC, T.rl[:, 0:18])
+    need(TE, "t", kc, ksc)
+    ks = layer(4, "xr", RC)
+    cx0 = pick_c("xx", 0, S, "w2", 0, 2 * S + 2 * RC, T.p2[:, 0:16])
+    sx0 = pick_s("xx", 0, S, "w2", 0, 2 * S + 2 * RC, T.p2[:, 0:16])
+    need(ACT, "a", ks[0])
+    kr = [relu(0, 4, RC, "hr")]
+    need(V, "v", ks[1])
+    kr.append(relu(1, 4, RC, "hr"))
+    cx1 = pick_c("xx", S, 2 * S, "w2", 0, 2 * S + 2 * RC, T.p2[:, 16:32])
+    sx1 = pick_s("xx", S, 2 * S, "w2", 0, 2 * S + 2 * RC, T.p2[:, 16:32])
+    need(ACT, "a", ks[2])
+    kr.append(relu(2, 4, RC, "hr"))
+    need(V, "v", ks[3])
+    kr.append(relu(3, 4, RC, "hr"))
+    need(V, "v", *kr)
+    k_hr = v(V.quantize_mx(T.hb_c[:, S:XT], T.hb_s[:, S:XT], T.hr[:]))
+
+    need(TE, "t", cx0, sx0, cx1, sx1, k_u, k_v, *kr)
+    for i in range(2):
+        for hf in range(2):
+            mm(T["ps%d" % hf][:, 0:128], "cu", 128 * i, "xx", S * i + 128 * hf, 128, i == 0, False)
+    need(V, "v", k_hr, k_ho)
+    need(ACT, "a", k_hr, k_ho)
+    ky = {}
+    for i in range(2):
+        kc = pick_c("hg", S * i, S * i + S, "hb", 0, XT, T.pu[:, 16 * i:16 * i + 16])
+        ksc = pick_s("hg", S * i, S * i + S, "hb", 0, XT, T.pu[:, 16 * i:16 * i + 16])
+        need(TE, "t", kc, ksc)
+        for hf in range(2):
+            ky[hf] = mm(T["ps%d" % hf][:, 0:128], "cv", 128 * i, "hg", S * i + 128 * hf, 128, False, i == 1)
+    need(V, "v", ky[0])
+    k = v(V.tensor_copy(T.yb[:, 0:128], T.ps0[:, 0:128]))
+    need(SY, "s", k)
+    SY.dma_start(T.y[:, 0:128], T.yb[:, 0:128]).then_inc(sem["y0"], 16)
+    need(ACT, "a", ky[1])
+    k = a(ACT.activation(T.yb[:, 128:256], T.ps1[:, 0:128], F.Copy))
+    need(ACT, "a", k)
+    ACT.dma_start(T.y[:, 128:256], T.yb[:, 128:256]).then_inc(sem["y1"], 16)
+
+    SY.wait_ge(sem["y0"], 16)
+    ACT.wait_ge(sem["y1"], 16)
+    g.wait_ge(sem["ls"], sent[0])
+    for name in ("sv", "sa", "st", "sp"):
+        g.wait_ge(sem[name], count[name])

@@ -1,4 +1,3 @@
-import numpy as np
 from concourse.bass import DstId, RemoteDMATransfer
 from concourse.mybir import dt, AluOpType, AxisListType, ActivationFunctionType
 
@@ -6,78 +5,27 @@ S = 256
 C1 = 48
 RC = 3 * C1
 XT = S + RC
-CODE = "float8_e4m3fn_x4"
+KW = 416
 
-SCRATCH = {
-    "nbi": ("sbuf", [128, 32], "int32"),
-    "w": ("sbuf", [128, 32], "uint16"),
-    "band": ("sbuf", [128, 1120], "bfloat16"),
-    "jd": ("sbuf", [128, 32], "float32"),
-    "li": ("sbuf", [128, 8], "int32"),
-    "lu": ("sbuf", [128, 8], "uint16"),
-    "ti": ("sbuf", [128, 2], "int32"),
-    "tq": ("sbuf", [128, 2], "int32"),
-    "thr": ("sbuf", [128, 4], "float32"),
-    "mi": ("sbuf", [128, 512], "int32"),
-    "mj": ("sbuf", [128, 512], "int32"),
-    "mask": ("sbuf", [128, 512], "float32"),
-    "rli": ("sbuf", [128, 18], "int32"),
-    "rl": ("sbuf", [128, 18], "uint16"),
-    "junk": ("sbuf", [128, 2048], "bfloat16"),
-    "cnt": ("sbuf", [128, 8], "float32"),
-    "cint": ("sbuf", [128, 8], "int32"),
-    "clo": ("sbuf", [128, 8], "int32"),
-    "fx": ("sbuf", [128, 256], "bfloat16"),
-    "fy": ("sbuf", [128, 256], "bfloat16"),
-    "dd": ("sbuf", [128, 256], "bfloat16"),
-    "jf": ("sbuf", [128, 512], "bfloat16"),
-    "jv": ("sbuf", [128, 256], "bfloat16"),
-    "ss": ("sbuf", [128, 4], "float32"),
-    "fu": ("sbuf", [128, 3], "uint16"),
-    "rf": ("sbuf", [128, 16], "uint16"),
-    "pm": ("sbuf", [128, 1024], "float32"),
-    "pf": ("sbuf", [128, 512], "float32"),
-    "m1": ("sbuf", [128, 512], "float32"),
-    "sb1": ("sbuf", [128, 528], "float32"),
-    "m2": ("sbuf", [128, 288], "float32"),
-    "sb2": ("sbuf", [128, 304], "float32"),
-    "cpi": ("sbuf", [128, 18], "int32"),
-    "cp": ("sbuf", [128, 18], "uint16"),
-    "pi": ("sbuf", [128, 32], "int32"),
-    "pu": ("sbuf", [128, 32], "uint16"),
-    "pt": ("sbuf", [128, 32], "int32"),
-    "pg": ("sbuf", [128, 32], "int32"),
-    "ptg": ("sbuf", [128, 32], "int32"),
-    "pq": ("sbuf", [128, 32], "int32"),
-    "pk": ("sbuf", [128, 16], "int32"),
-    "pr": ("sbuf", [128, 32], "int32"),
-    "p2": ("sbuf", [128, 32], "uint16"),
-    "xt": ("sbuf", [128, 1024], "bfloat16"),
-    "at": ("sbuf", [128, 4096], "bfloat16"),
-    "vt": ("sbuf", [128, 1024], "bfloat16"),
-    "ut": ("sbuf", [128, 1024], "bfloat16"),
-    "ho": ("sbuf", [128, 1024], "bfloat16"),
-    "hr": ("sbuf", [128, 4 * RC], "bfloat16"),
-    "yb": ("sbuf", [128, 256], "float32"),
-}
-for _n, _w in (("ca", 1024), ("cv", 256), ("cu", 256),
-               ("x0", S),
-               ("s1", RC),
-               ("xb", XT),
-               ("s2", 2 * RC),
-               ("w2", 2 * S + 2 * RC),
-               ("xr", 2 * RC),
-               ("xx", 2 * S),
-               ("hb", XT),
-               ("hg", 2 * S)):
-    SCRATCH[_n + "_c"] = ("sbuf", [128, _w], CODE)
+SCRATCH = {}
+for _t, _l in (("int32", "nbi32 li8 ti2 tq2 rli20 cint4 clo4"),
+               ("uint16", "w32 lu8 rl20 fu3 rf16 cp18 pu32"),
+               ("bfloat16", "band1120 mi512 mask512 rs512 junk2048 fx256 fy256 dd256 jf512 jv256 pm1024 pf512 ma512 sba512 "
+                            "mb288 sbb288 xt1024 at4096 vt1024 ut512 ho1024 hr576"),
+               ("float32", "jd32 thr4 cnt4 cnv4 gh8 gl8 ss4 yb256")):
+    for _e in _l.split():
+        _n = _e.rstrip("0123456789")
+        SCRATCH[_n] = ("sbuf", [128, int(_e[len(_n):])], _t)
+for _n, _w in (("ca", 1024), ("cv", 256), ("cu", 256), ("x0", S), ("s1", RC), ("xb", XT), ("s2", 2 * RC), ("l2", 2 * RC),
+               ("w2", KW + XT), ("xx", 2 * S), ("hb", XT), ("hg", 2 * S)):
+    SCRATCH[_n + "_c"] = ("sbuf", [128, _w], "float8_e4m3fn_x4")
     SCRATCH[_n + "_s"] = ("sbuf", [128, _w], "uint8")
 for _i in range(8):
     SCRATCH["ps%d" % _i] = ("psum", [128, 512], "float32")
-
 SEMAPHORES = ["sv", "sa", "st", "sp",
-              "ln", "lx", "la0", "la1", "lu_", "lv_",
-              "rq", "xc", "xs", "bc", "bs", "ls",
+              "ln", "lx", "la0", "la1", "lu_", "lv_", "lb",
+              "uc", "us", "rq", "xc", "xs", "bc", "bs",
+              "lq", "lf", "ls",
               "y0", "y1"]
 
 
@@ -85,8 +33,7 @@ def rank_program(g, core, T, topo):
     rank = T.rank_of(core)
     if rank is None:
         return
-    A = AluOpType
-    F = ActivationFunctionType
+    A, F, X = AluOpType, ActivationFunctionType, AxisListType.X
     V, ACT, TE, SY = g.vector, g.scalar, g.tensor, g.sync
     sem = T.sem
     cores = list(T.cores)
@@ -105,12 +52,6 @@ def rank_program(g, core, T, topo):
     def a(ins):
         return done("sa", ins)
 
-    def t(ins):
-        return done("st", ins)
-
-    def p(ins):
-        return done("sp", ins)
-
     def need(eng, tag, *marks):
         best = {}
         for name, c in marks:
@@ -120,42 +61,64 @@ def rank_program(g, core, T, topo):
                 eng.wait_ge(sem[name], c)
                 seen[tag, name] = c
 
+    def nv(*marks):
+        need(V, "v", *marks)
+
+    def na(*marks):
+        need(ACT, "a", *marks)
+
+    def iota(out, pattern, base=0, step=0, whole=False):
+        if whole:
+            return done("sp", g.iota(out, pattern, base, step))
+        return done("sp", g.iota(out, pattern, base, step, allow_small_or_imprecise_dtypes=True))
+
     def others(r):
         return [q for q in range(n) if q != r]
 
+    def near(r):
+        return [q for q in others(r) if topo.chip(cores[q]) == topo.chip(cores[r])]
+
     def lanes(r):
         me = cores[r]
-        off = [q for q in others(r) if topo.chip(cores[q]) != topo.chip(me)]
-        on = [q for q in others(r) if topo.chip(cores[q]) == topo.chip(me)]
+        off = [q for q in others(r) if q not in near(r)]
         res, used = {}, []
         for i, q in enumerate(off):
             e = topo.engines(me, cores[q])
             k = len(e) // len(off)
             res[q] = e[i * k:(i + 1) * k]
             used += res[q]
-        for i, q in enumerate(on):
+        for i, q in enumerate(near(r)):
             e = [x for x in topo.engines(me, cores[q]) if x not in used]
-            res[q] = e[i::2 * len(on)]
-        return res
+            res[q] = e[i::2 * len(near(r))]
+        return res, used
 
-    lane = lanes(rank)
-    into = sum(len(lanes(q)[rank]) for q in others(rank))
-    sent = [0]
+    lane, away = lanes(rank)
+    into = sum(len(lanes(q)[0][rank]) for q in others(rank))
+    mate = near(rank)[0]
+    half = 128 * (rank > mate)
+    sent = {"lq": 0, "lf": 0, "ls": 0}
 
-    def send(pieces, rsem):
+    def send(pieces, rsem, lsem="lq"):
         tr = []
-        for q, (src, dst) in pieces.items():
+        for q, engines, src, dst in pieces:
             rid, pid, _ = topo.addr(cores[q])
-            m = 0
-            for e in lane[q]:
-                m |= 1 << e
-            tr.append(RemoteDMATransfer(dst_ids=[DstId(rid=rid, pnc=pid)], dma_engine_mask=m, remote_sem=sem[rsem],
-                                        src=src, dst=dst, alu_op=0))
-            sent[0] += len(lane[q])
-        g.remote_dma_fused(tr, local_sem=sem["ls"])
+            tr.append(RemoteDMATransfer(dst_ids=[DstId(rid=rid, pnc=pid)], dma_engine_mask=sum(1 << e for e in engines),
+                                        remote_sem=sem[rsem], src=src, dst=dst, alu_op=0))
+            sent[lsem] += len(engines)
+        g.remote_dma_fused(tr, local_sem=sem[lsem])
 
     def codes(name, lo, hi):
         return T[name + "_c"][:, lo:hi].bitcast(dt.uint8)
+
+    def scales(name, lo, hi):
+        return T[name + "_s"][:, lo:hi]
+
+    def deal(kind, src, dst, first, size, rsem, lsem):
+        out = []
+        for q in others(rank):
+            i, j = size * others(rank).index(q), first + size * others(q).index(rank)
+            out.append((q, lane[q], kind(src, i, i + size), kind(dst, j, j + size)))
+        send(out, rsem, lsem)
 
     def pick_c(out, lo, hi, win, wlo, whi, off):
         return v(V.tensor_copy(T[out + "_c"][:, lo:hi].bitcast(dt.uint32),
@@ -164,257 +127,257 @@ def rank_program(g, core, T, topo):
     def pick_s(out, lo, hi, win, wlo, whi, off):
         return a(ACT.activation(T[out + "_s"][:, lo:hi], T[win + "_s"][:, wlo:whi].indirect(off), F.Copy))
 
-    def quad(q):
-        return 32 * q, 32 * q + 32
+    def pick_sv(out, lo, hi, win, wlo, whi, off):
+        return v(V.tensor_copy(T[out + "_s"][:, lo:hi], T[win + "_s"][:, wlo:whi].indirect(off)))
 
-    SY.dma_start(T.nbi[0:16, 0:16], T.nb0[:]).then_inc(sem["ln"], 16)
-    ACT.dma_start(T.nbi[0:16, 16:32], T.nb1[:]).then_inc(sem["ln"], 16)
-    SY.dma_start(T.nbi[16:32, 0:16], T.nb0[:]).then_inc(sem["ln"], 16)
-    ACT.dma_start(T.nbi[16:32, 16:32], T.nb1[:]).then_inc(sem["ln"], 16)
+    def pack(name, lo, hi, src):
+        return v(V.quantize_mx(T[name + "_c"][:, lo:hi], T[name + "_s"][:, lo:hi], src))
+
+    def quad(q):
+        return slice(32 * q, 32 * q + 32)
+
+    for r in (0, 16):
+        SY.dma_start(T.nbi[r:r + 16, 0:16], T.nb0[:]).then_inc(sem["ln"], 16)
+        ACT.dma_start(T.nbi[r:r + 16, 16:32], T.nb1[:]).then_inc(sem["ln"], 16)
+    SY.dma_start(T.ut[:], T.u[:, 4 * half:4 * half + 512]).then_inc(sem["lu_"], 16)
     SY.dma_start(T.xt[:], T.x[:]).then_inc(sem["lx"], 16)
     SY.dma_start(T.at[:, 0:2048], T.a[:, 0:2048]).then_inc(sem["la0"], 16)
     SY.dma_start(T.at[:, 2048:4096], T.a[:, 2048:4096]).then_inc(sem["la1"], 16)
-    SY.dma_start(T.ut[:], T.u[:]).then_inc(sem["lu_"], 16)
-    SY.dma_start(T.vt[:], T.v[:]).then_inc(sem["lv_"], 16)
 
-    k_jd = p(g.iota(T.jd[:], [[1, 32]], 0, -1, allow_small_or_imprecise_dtypes=True))
-    k_li = p(g.iota(T.li[:], [[1, 4], [0, 2]], 0, 0))
-    k_ti = p(g.iota(T.ti[:], [[0, 2]], 0, 1))
-    k_mi = p(g.iota(T.mi[:], [[0, 32], [1, 16]], 128, -1))
-    k_rl = p(g.iota(T.rli[:], [[16, 2], [32, 9]], 0, 0))
-    k_po = p(g.iota(T.pm[:, S * rank:S * rank + S], [[1, S]], 0, 0, allow_small_or_imprecise_dtypes=True))
-
+    k_jd = iota(T.jd[:], [[1, 32]], 0, -1)
+    iota(T.ti[:], [[0, 2]], 0, 1, whole=True)
+    k_li = iota(T.li[:], [[1, 4], [0, 2]], whole=True)
+    iota(T.cnt[:], [[0, 4]])
+    iota(T.cnv[:], [[0, 4]])
+    k_cn = iota(T.jv[:, 240:256], [[0, 16]], -255)
+    iota(T.rli[:], [[16, 2], [32, 10]], whole=True)
+    iota(T.mi[:], [[0, 32], [1, 16]])
     k = v(V.memset(T.band[:], 0.0))
-    need(V, "v", k, k_jd)
+    nv(k, k_jd)
     for q in range(n):
-        lo, hi = quad(q)
-        c = 96 + S * q
-        v(V.tensor_scalar(T.band[lo:hi, c:c + 32], T.jd[lo:hi, :], float(-lo), None, A.is_equal))
-        k_band = v(V.tensor_scalar(T.band[lo:hi, c + 128:c + 160], T.jd[lo:hi, :], float(-lo), 1024.0, A.is_equal, A.mult))
-    need(V, "v", k_ti)
-    k_l = v(V.tensor_copy(T.lu[:], T.li[:]))
+        c, z = 96 + S * q, float(-32 * q)
+        v(V.tensor_scalar(T.band[quad(q), c:c + 32], T.jd[quad(q), :], z, None, A.is_equal))
+        v(V.tensor_scalar(T.band[quad(q), c + 128:c + 160], T.jd[quad(q), :], z, 1024.0, A.is_equal, A.mult))
+    nv(k_li)
     k = v(V.tensor_scalar(T.tq[:], T.ti[:], 15, None, A.bitwise_and))
-    v(V.memset(T.jv[:, 240:256], -255.0))
-    v(V.memset(T.sb1[:, 0:16], 0.0))
-    v(V.memset(T.sb2[:, 0:16], 0.0))
-    need(V, "v", k)
+    v(V.tensor_copy(T.lu[:], T.li[:]))
+    nv(k)
     for c in range(3):
-        k_thr = v(V.tensor_scalar(T.thr[:, c:c + 1], T.tq[:, 0:1], 16 * c + 0.5, None, A.add))
+        v(V.tensor_scalar(T.thr[:, c:c + 1], T.tq[:, 0:1], 16 * c + 0.5, None, A.add))
 
     V.wait_ge(sem["ln"], 64)
     for q in range(n):
-        lo, hi = quad(q)
-        k_w = v(V.tensor_copy(T.w[lo:hi, :], T.nbi[0:32, :]))
-    need(ACT, "a", k_w)
+        k_w = v(V.tensor_copy(T.w[quad(q), :], T.nbi[0:32, :]))
+    na(k_w, k_cn)
     for i in range(3):
-        k_ca = a(ACT.activation(T.junk[:, 512 * i:512 * i + 512], T.band[:, 96 - 32 * i:1120 - 32 * i].indirect(T.w[:, 0:32]),
+        e = 32 if i < 2 else 16
+        k_ca = a(ACT.activation(T.junk[:, 512 * i:512 * i + 16 * e],
+                                T.band[:, 96 - 32 * i:1120 - 32 * i].indirect(T.w[:, 0:e]),
                                 F.Copy, accum_out=T.cnt[:, i:i + 1]))
-    need(V, "v", k_w)
-    k = v(V.tensor_copy(T.junk[:, 1536:2048], T.band[:, 0:1024].indirect(T.w[:, 0:32])))
-    need(V, "v", k)
-    k_cv = v(V.tensor_reduce(T.cnt[:, 3:4], T.junk[:, 1536:2048], AxisListType.X, A.add))
-    need(V, "v", k_cv, k_ca, k_l)
-    k = v(V.tensor_copy(T.cint[:, 0:4], T.cnt[:, 0:4]))
-    k_h = v(V.tensor_scalar(T.fx[:, 128:256], T.cnt[:, 0:4].indirect(T.lu[:, 0:8]), 1023.5, None, A.is_ge))
-    need(V, "v", k)
-    k = v(V.tensor_scalar(T.clo[:, 0:4], T.cint[:, 0:4], 1023, None, A.bitwise_and))
-    need(V, "v", k)
-    k = v(V.tensor_scalar(T.fx[:, 0:128], T.clo[:, 0:4].indirect(T.lu[:, 0:8]), 0.5, None, A.is_ge))
-    need(V, "v", k, k_h)
+    nv(k_w, k_cn)
+    k3 = v(V.tensor_copy(T.junk[:, 1536:2048], T.band[:, 0:1024].indirect(T.w[:, 0:32])))
+    k2 = v(V.tensor_copy(T.junk[:, 1280:1536], T.band[:, 32:1056].indirect(T.w[:, 16:32])))
+    V.wait_ge(sem["lu_"], 16)
+    k_u = pack("cu", half, half + 128, T.ut[:])
+    nv(k3)
+    v(V.tensor_reduce(T.cnv[:, 3:4], T.junk[:, 1536:2048], X, A.add))
+    nv(k2)
+    k_cv = v(V.tensor_reduce(T.cnv[:, 2:3], T.junk[:, 1280:1536], X, A.add))
+    need(g, "g", k_u)
+    send([(mate, away, codes("cu", half, half + 128), codes("cu", half, half + 128))], "uc")
+    send([(mate, lane[mate], scales("cu", half, half + 128), scales("cu", half, half + 128))], "us")
+    k_mi = iota(T.pm[:, S * rank:S * rank + S], [[1, S]], -S)
+    nv(k_cv, k_ca)
+    k = v(V.tensor_tensor(T.cint[:], T.cnt[:], T.cnv[:], A.add))
+    nv(k)
+    k_gh = v(V.tensor_scalar(T.gh[:, 0:4], T.cint[:], 1023.5, None, A.is_ge))
+    k = v(V.tensor_scalar(T.clo[:], T.cint[:], 1023, None, A.bitwise_and))
+    nv(k)
+    k = v(V.tensor_scalar(T.gl[:, 0:4], T.clo[:], 0.5, None, A.is_ge))
+    na(k_gh)
+    k_h = a(ACT.activation(T.fx[:, 128:256], T.gh[:, 0:4].indirect(T.lu[:, 0:8]), F.Copy))
+    nv(k)
+    k = v(V.tensor_copy(T.fx[:, 0:128], T.gl[:, 0:4].indirect(T.lu[:, 0:8])))
+    nv(k, k_h)
     k = v(V.transpose(T.fy[:], T.fx[:]))
-    need(V, "v", k)
+    nv(k)
     k_d = v(V.tensor_tensor_scan(T.dd[:], T.fy[:], T.fy[:], 0.0, A.add, A.max))
-    need(ACT, "a", k_d)
+    na(k_d)
     for c in range(2):
         k_sa = a(ACT.activation(T.jf[:, 256 * c:256 * c + 255], T.dd[:, 0:255], F.Sign, bias=T.thr[:, c:c + 1], scale=-1.0,
                                 accum_out=T.ss[:, c:c + 1]))
-    need(V, "v", k_d)
+    nv(k_d)
     k = v(V.tensor_scalar(T.jv[:, 0:255], T.dd[:, 0:255], T.thr[:, 2:3], 2.0, A.is_le, A.mult))
-    need(V, "v", k)
-    k = v(V.tensor_reduce(T.ss[:, 2:3], T.jv[:], AxisListType.X, A.add))
-    need(V, "v", k, k_sa)
+    nv(k)
+    k = v(V.tensor_reduce(T.ss[:, 2:3], T.jv[:], X, A.add))
+    nv(k, k_sa)
     k_fu = v(V.tensor_scalar(T.fu[:], T.ss[:, 0:3], 255.0, 0.5, A.add, A.mult))
 
     need(g, "g", k_fu)
-    send({q: (T.fu[:], T.rf[:, 3 * others(q).index(rank):3 * others(q).index(rank) + 3]) for q in others(rank)}, "rq")
+    send([(q, lane[q], T.fu[:], T.rf[:, 3 * others(q).index(rank):3 * others(q).index(rank) + 3]) for q in others(rank)], "rq")
 
     V.wait_ge(sem["lx"], 16)
-    k_x0 = v(V.quantize_mx(T.x0_c[:], T.x0_s[:], T.xt[:]))
-    k_xb = v(V.quantize_mx(T.xb_c[:, 0:S], T.xb_s[:, 0:S], T.xt[:]))
+    k_x0 = pack("x0", 0, S, T.xt[:])
+    SY.wait_ge(sem["lq"], sent["lq"])
+    need(SY, "s", k_x0)
+    SY.dma_start(codes("xb", 0, S), codes("x0", 0, S)).then_inc(sem["lb"], 16)
+    SY.dma_start(scales("xb", 0, S), scales("x0", 0, S)).then_inc(sem["lb"], 16)
     turn = 0
-    k_pm = []
+    k_pm = [k_mi]
     for i, q in enumerate(others(rank)):
-        ql, qh = quad(q)
-        base = float(S - 1 + C1 * i)
+        base = float(C1 * i - 1)
         for z in range(n):
-            lo, hi = quad(z)
-            out = T.pm[lo:hi, S * q:S * q + S]
-            if turn % 3 == 0:
-                k_pm.append(v(V.tensor_scalar(out, T.dd[ql:qh, :], base, None, A.add)))
+            out = T.pm[quad(z), S * q:S * q + S]
+            if turn % 2 == 0:
+                k_pm.append(v(V.tensor_scalar(out, T.dd[quad(q), :], base, None, A.add)))
             else:
-                k_pm.append(a(ACT.activation(out, T.dd[ql:qh, :], F.Copy, bias=base)))
+                k_pm.append(a(ACT.activation(out, T.dd[quad(q), :], F.Copy, bias=base)))
             turn += 1
-    need(V, "v", k_mi)
-    k = v(V.tensor_scalar(T.mj[:], T.mi[:], 15, None, A.bitwise_and))
-    need(V, "v", k)
-    k_mask = v(V.tensor_scalar(T.mask[:], T.mj[:], 0.0, None, A.is_equal))
+    na(*k_pm)
+    k_pf = a(ACT.activation(T.pf[:], T.pm[:].indirect(T.w[:, 0:32]), F.Copy))
+    nv(k_mi)
+    v(V.tensor_scalar(T.mask[:], T.mi[:], 0.5, T.thr[:, 0:1], A.add, A.is_equal))
+    v(V.tensor_scalar(T.rs[:], T.mi[:], 0.5, None, A.is_ge))
+    v(V.tensor_scalar(T.rl[:], T.rli[:], T.thr[:, 0:1], -0.5, A.add, A.add))
     V.wait_ge(sem["la0"], 16)
-    k_a0 = v(V.quantize_mx(T.ca_c[:, 0:512], T.ca_s[:, 0:512], T.at[:, 0:2048]))
+    k_a0 = pack("ca", 0, 512, T.at[:, 0:2048])
 
     V.wait_ge(sem["rq"], into)
-    sl, sh = quad(rank)
-    for z in range(n):
-        if z != rank:
-            lo, hi = quad(z)
-            k_rf = v(V.tensor_copy(T.rf[lo:hi, 0:9], T.rf[sl:sh, 0:9]))
-    need(V, "v", k_rf, k_x0)
+    for z in others(rank):
+        k_rf = v(V.tensor_copy(T.rf[quad(z), 0:9], T.rf[quad(rank), 0:9]))
+    nv(k_rf)
     k_c = pick_c("s1", 0, RC, "x0", 0, S, T.rf[:, 0:9])
-    need(ACT, "a", k_rf, k_x0)
+    na(k_rf)
     k_s = pick_s("s1", 0, RC, "x0", 0, S, T.rf[:, 0:9])
-
-    def at(q, size):
-        i, j = others(rank).index(q), others(q).index(rank)
-        return size * i, size * j
-
     need(g, "g", k_c)
-    send({q: (codes("s1", at(q, C1)[0], at(q, C1)[0] + C1), codes("xb", S + at(q, C1)[1], S + at(q, C1)[1] + C1))
-          for q in others(rank)}, "xc")
+    deal(codes, "s1", "xb", S, C1, "xc", "lf")
     need(g, "g", k_s)
-    send({q: (T.s1_s[:, at(q, C1)[0]:at(q, C1)[0] + C1], T.xb_s[:, S + at(q, C1)[1]:S + at(q, C1)[1] + C1])
-          for q in others(rank)}, "xs")
+    deal(scales, "s1", "xb", S, C1, "xs", "lf")
+    SY.wait_ge(sem["lf"], sent["lf"])
+    SY.dma_start(T.vt[:], T.v[:]).then_inc(sem["lv_"], 16)
 
-    need(ACT, "a", k_po, *k_pm)
-    k_pf = a(ACT.activation(T.pf[:], T.pm[:].indirect(T.w[:, 0:32]), F.Copy))
-    need(V, "v", k_mask, k_po, *k_pm)
-    k_m1 = v(V.tensor_tensor(T.m1[:], T.pm[:].indirect(T.w[:, 0:32]), T.mask[:], A.mult))
-    need(V, "v", k_pf)
+    nv(k_c, k_pf, *k_pm)
+    v(V.tensor_tensor(T.ma[:], T.pm[:].indirect(T.w[:, 0:32]), T.mask[:], A.mult))
     for i in range(2):
-        k = v(V.tensor_tensor(T.m2[:, RC * i:RC * i + RC], T.pf[:, S * i:S * i + S].indirect(T.rf[:, 0:9]), T.mask[:, 0:RC],
+        k = v(V.tensor_tensor(T.mb[:, RC * i:RC * i + RC], T.pf[:, S * i:S * i + S].indirect(T.rf[:, 0:9]), T.mask[:, 0:RC],
                               A.mult))
-    need(V, "v", k)
-    k = v(V.tensor_tensor_scan(T.sb2[:, 16:304], T.m2[:], T.m2[:], 0.0, A.add, A.max))
-    k_sb1 = v(V.tensor_tensor_scan(T.sb1[:, 16:528], T.m1[:], T.m1[:], 0.0, A.add, A.max))
-    need(V, "v", k)
+    nv(k)
+    k = v(V.tensor_tensor_scan(T.sbb[:], T.rs[:, 0:2 * RC], T.mb[:], 0.0, A.mult, A.add))
+    k_sa = v(V.tensor_tensor_scan(T.sba[:], T.rs[:], T.ma[:], 0.0, A.mult, A.add))
+    nv(k)
     for i in range(2):
-        e = 15 + RC * i
-        k = v(V.tensor_tensor(T.cpi[:, i:18:2], T.sb2[:, e + 16:e + 16 + 129:16], T.sb2[:, e:e + 129:16], A.subtract))
-    need(V, "v", k)
-    k_cp = v(V.tensor_copy(T.cp[:], T.cpi[:]))
-    k_pi = v(V.tensor_tensor(T.pi[:], T.sb1[:, 31:528:16], T.sb1[:, 15:512:16], A.subtract))
-    need(V, "v", k_pi)
-    k_pu = v(V.tensor_copy(T.pu[:], T.pi[:]))
-    V.wait_ge(sem["la1"], 16)
-    k_a1 = v(V.quantize_mx(T.ca_c[:, 512:1024], T.ca_s[:, 512:1024], T.at[:, 2048:4096]))
+        v(V.tensor_scalar(T.cp[:, i:18:2], T.sbb[:, RC * i + 15:RC * i + RC:16], float(S), None, A.add))
+    nv(k_sa)
+    k_pu = v(V.tensor_scalar(T.pu[:], T.sba[:, 15:512:16], float(S), None, A.add))
 
+    V.wait_ge(sem["lb"], 32)
     V.wait_ge(sem["xc"], into)
-    need(V, "v", k_cp, k_pu, k_xb)
-    k_c = pick_c("s2", 0, 2 * RC, "xb", 0, XT, T.cp[:, 0:18])
+    nv(k_pu)
+    pick_c("s2", 0, 160, "xb", 0, XT, T.cp[:, 0:10])
+    k_c = pick_c("s2", 160, 2 * RC, "xb", 0, XT, T.cp[:, 10:18])
+    cw0 = pick_c("w2", 0, S, "xb", 0, XT, T.pu[:, 0:16])
+    ACT.wait_ge(sem["lb"], 32)
     ACT.wait_ge(sem["xs"], into)
-    need(ACT, "a", k_cp, k_pu, k_xb)
-    k_s = pick_s("s2", 0, 2 * RC, "xb", 0, XT, T.cp[:, 0:18])
-    W = 2 * C1
+    na(k_pu)
+    k_s0 = pick_s("s2", 0, 160, "xb", 0, XT, T.cp[:, 0:10])
+    V.wait_ge(sem["xs"], into)
+    k_s1 = pick_sv("s2", 160, 2 * RC, "xb", 0, XT, T.cp[:, 10:18])
     need(g, "g", k_c)
-    send({q: (codes("s2", at(q, W)[0], at(q, W)[0] + W), codes("w2", 2 * S + at(q, W)[1], 2 * S + at(q, W)[1] + W))
-          for q in others(rank)}, "bc")
-    need(g, "g", k_s)
-    send({q: (T.s2_s[:, at(q, W)[0]:at(q, W)[0] + W], T.w2_s[:, 2 * S + at(q, W)[1]:2 * S + at(q, W)[1] + W])
-          for q in others(rank)}, "bs")
+    deal(codes, "s2", "l2", 0, 2 * C1, "bc", "ls")
+    need(g, "g", k_s0, k_s1)
+    deal(scales, "s2", "l2", 0, 2 * C1, "bs", "ls")
 
-    k_c = pick_c("w2", 0, 2 * S, "xb", 0, XT, T.pu[:, 0:32])
-    k_s = pick_s("w2", 0, 2 * S, "xb", 0, XT, T.pu[:, 0:32])
+    cw1 = pick_c("w2", KW, KW + S, "xb", 0, XT, T.pu[:, 16:32])
+    sw0 = pick_s("w2", 0, S, "xb", 0, XT, T.pu[:, 0:16])
+    sw1 = pick_s("w2", KW, KW + S, "xb", 0, XT, T.pu[:, 16:32])
 
     def mm(out, wt, wcol, mv, c, width, start, stop):
-        return t(TE.matmul_mx(out, T[wt + "_c"][:, wcol:wcol + 128], T[wt + "_s"][:, wcol:wcol + 128],
-                              T[mv + "_c"][:, c:c + width], T[mv + "_s"][:, c:c + width], start, stop))
+        return done("st", TE.matmul_mx(out, T[wt + "_c"][:, wcol:wcol + 128], T[wt + "_s"][:, wcol:wcol + 128],
+                                       T[mv + "_c"][:, c:c + width], T[mv + "_s"][:, c:c + width], start, stop))
 
-    def layer(bank, mv, width):
-        ks = []
-        for b in range(4):
-            out = T["ps%d" % (bank + b)][:, 0:width]
-            mm(out, "ca", 128 * b, mv, 0, width, True, False)
-            ks.append(mm(out, "ca", 512 + 128 * b, mv, width, width, False, True))
-        return ks
-
-    def relu(b, bank, width, tile):
+    def relu(b, bank, width, tile, on_vector):
         out = T[tile][:, b:4 * width:4]
         src = T["ps%d" % (bank + b)][:, 0:width]
-        if b % 2:
+        if on_vector:
             return v(V.tensor_scalar(out, src, 0.0, 0.05, A.max, A.mult))
         return a(ACT.activation(out, src, F.Relu, scale=0.05))
 
-    need(TE, "t", k_c, k_s, k_a0, k_a1)
-    ks = layer(0, "w2", S)
-    k_t = v(V.tensor_scalar(T.pt[:], T.pi[:], 1008, None, A.bitwise_and))
-    k_g = v(V.tensor_scalar(T.pg[:], T.pi[:], float(S), None, A.is_ge))
-    need(V, "v", k_t, k_g)
-    k = v(V.tensor_tensor(T.ptg[:], T.pt[:], T.pg[:], A.mult))
-    v(V.tensor_scalar(T.pk[:], T.pg[:, 16:32], float(16 - S), float(S), A.mult, A.add))
-    need(V, "v", k)
-    k = v(V.tensor_tensor(T.pq[:], T.pi[:], T.ptg[:], A.add))
-    need(V, "v", k)
-    k_p2 = v(V.tensor_copy(T.p2[:, 0:16], T.pq[:, 0:16]))
-    k = v(V.tensor_tensor(T.pr[:, 16:32], T.pq[:, 16:32], T.pk[:], A.add))
-    need(V, "v", k, k_rl)
-    k_p2 = v(V.tensor_copy(T.p2[:, 16:32], T.pr[:, 16:32]))
-    k_rlu = v(V.tensor_scalar(T.rl[:], T.rli[:], T.thr[:, 0:1], -0.5, A.add, A.add))
-    V.wait_ge(sem["lu_"], 16)
-    k_u = v(V.quantize_mx(T.cu_c[:], T.cu_s[:], T.ut[:]))
-    V.wait_ge(sem["lv_"], 16)
-    k_v = v(V.quantize_mx(T.cv_c[:], T.cv_s[:], T.vt[:]))
-    kr = []
+    V.wait_ge(sem["la1"], 16)
+    k_a1 = pack("ca", 512, 1024, T.at[:, 2048:4096])
+    need(TE, "t", cw0, sw0, k_a0)
     for b in range(4):
-        need(*((V, "v") if b % 2 else (ACT, "a")), ks[b])
-        kr.append(relu(b, 0, S, "ho"))
-    need(V, "v", *kr)
-    k_ho = v(V.quantize_mx(T.hb_c[:, 0:S], T.hb_s[:, 0:S], T.ho[:]))
+        mm(T["ps%d" % b][:, 0:S], "ca", 128 * b, "w2", 0, S, True, False)
+    need(TE, "t", cw1, sw1, k_a1)
+    ks = [mm(T["ps%d" % b][:, 0:S], "ca", 512 + 128 * b, "w2", KW, S, False, True) for b in range(4)]
+    k_ro = []
+    for b in range(4):
+        na(ks[b])
+        k_ro.append(relu(b, 0, S, "ho", False))
 
     V.wait_ge(sem["bc"], into)
-    need(V, "v", k_rlu, k_p2)
-    kc = pick_c("xr", 0, 2 * RC, "w2", 2 * S, 2 * S + 2 * RC, T.rl[:, 0:18])
+    kc0 = pick_c("w2", S, XT, "l2", 0, 2 * RC, T.rl[:, 0:9])
+    kc1 = pick_c("w2", KW + S, KW + XT, "l2", 0, 2 * RC, T.rl[:, 10:19])
+    nv(kc0)
+    pick_c("xx", 0, S, "w2", 0, XT, T.pu[:, 0:16])
+    V.wait_ge(sem["bs"], into)
+    k1 = pick_sv("w2", KW + S, KW + XT, "l2", 0, 2 * RC, T.rl[:, 10:19])
     ACT.wait_ge(sem["bs"], into)
-    need(ACT, "a", k_rlu, k_p2)
-    ksc = pick_s("xr", 0, 2 * RC, "w2", 2 * S, 2 * S + 2 * RC, T.rl[:, 0:18])
-    need(TE, "t", kc, ksc)
-    ks = layer(4, "xr", RC)
-    cx0 = pick_c("xx", 0, S, "w2", 0, 2 * S + 2 * RC, T.p2[:, 0:16])
-    sx0 = pick_s("xx", 0, S, "w2", 0, 2 * S + 2 * RC, T.p2[:, 0:16])
-    need(ACT, "a", ks[0])
-    kr = [relu(0, 4, RC, "hr")]
-    need(V, "v", ks[1])
-    kr.append(relu(1, 4, RC, "hr"))
-    cx1 = pick_c("xx", S, 2 * S, "w2", 0, 2 * S + 2 * RC, T.p2[:, 16:32])
-    sx1 = pick_s("xx", S, 2 * S, "w2", 0, 2 * S + 2 * RC, T.p2[:, 16:32])
-    need(ACT, "a", ks[2])
-    kr.append(relu(2, 4, RC, "hr"))
-    need(V, "v", ks[3])
-    kr.append(relu(3, 4, RC, "hr"))
-    need(V, "v", *kr)
-    k_hr = v(V.quantize_mx(T.hb_c[:, S:XT], T.hb_s[:, S:XT], T.hr[:]))
+    k0 = pick_s("w2", S, XT, "l2", 0, 2 * RC, T.rl[:, 0:9])
+    need(TE, "t", kc1, k0, k1)
+    ks = []
+    for b in range(4):
+        out = T["ps%d" % (4 + b)][:, 0:RC]
+        mm(out, "ca", 128 * b, "w2", S, RC, True, False)
+        ks.append(mm(out, "ca", 512 + 128 * b, "w2", KW + S, RC, False, True))
+    na(k0)
+    pick_s("xx", 0, S, "w2", 0, XT, T.pu[:, 0:16])
+    V.wait_ge(sem["lv_"], 16)
+    k_v = pack("cv", 0, S, T.vt[:])
+    nv(kc1)
+    cx1 = pick_c("xx", S, 2 * S, "w2", KW, KW + XT, T.pu[:, 16:32])
+    na(ks[0])
+    kr = [relu(0, 4, RC, "hr", False)]
+    nv(ks[1])
+    kr.append(relu(1, 4, RC, "hr", True))
+    na(k1)
+    sx1 = pick_s("xx", S, 2 * S, "w2", KW, KW + XT, T.pu[:, 16:32])
+    nv(*k_ro)
+    pack("hb", 0, S, T.ho[:])
+    na(ks[2])
+    kr.append(relu(2, 4, RC, "hr", False))
+    nv(ks[3])
+    kr.append(relu(3, 4, RC, "hr", True))
+    nv(*kr)
+    k_hr = pack("hb", S, XT, T.hr[:])
 
-    need(TE, "t", cx0, sx0, cx1, sx1, k_u, k_v, *kr)
+    TE.wait_ge(sem["uc"], len(lanes(mate)[1]))
+    TE.wait_ge(sem["us"], len(lanes(mate)[0][rank]))
+    need(TE, "t", cx1, sx1, k_u, k_v, *k_ro)
     for i in range(2):
         for hf in range(2):
             mm(T["ps%d" % hf][:, 0:128], "cu", 128 * i, "xx", S * i + 128 * hf, 128, i == 0, False)
-    need(V, "v", k_hr, k_ho)
-    need(ACT, "a", k_hr, k_ho)
-    ky = {}
-    for i in range(2):
-        kc = pick_c("hg", S * i, S * i + S, "hb", 0, XT, T.pu[:, 16 * i:16 * i + 16])
-        ksc = pick_s("hg", S * i, S * i + S, "hb", 0, XT, T.pu[:, 16 * i:16 * i + 16])
-        need(TE, "t", kc, ksc)
-        for hf in range(2):
-            ky[hf] = mm(T["ps%d" % hf][:, 0:128], "cv", 128 * i, "hg", S * i + 128 * hf, 128, False, i == 1)
-    need(V, "v", ky[0])
-    k = v(V.tensor_copy(T.yb[:, 0:128], T.ps0[:, 0:128]))
-    need(SY, "s", k)
-    SY.dma_start(T.y[:, 0:128], T.yb[:, 0:128]).then_inc(sem["y0"], 16)
-    need(ACT, "a", ky[1])
+    nv(k_hr)
+    na(k_hr)
+    ky = []
+    for hf in range(2):
+        for i in range(2):
+            c, o = S * i + 128 * hf, 16 * i + 8 * hf
+            kc = pick_c("hg", c, c + 128, "hb", 0, XT, T.pu[:, o:o + 8])
+            ksc = pick_s("hg", c, c + 128, "hb", 0, XT, T.pu[:, o:o + 8])
+            need(TE, "t", kc, ksc)
+            ky.append(mm(T["ps%d" % hf][:, 0:128], "cv", 128 * i, "hg", c, 128, False, i == 1))
+            if len(ky) == 3:
+                nv(ky[1])
+                k = v(V.tensor_copy(T.yb[:, 0:128], T.ps0[:, 0:128]))
+                need(SY, "s", k)
+                SY.dma_start(T.y[:, 0:128], T.yb[:, 0:128]).then_inc(sem["y0"], 16)
+    na(ky[3])
     k = a(ACT.activation(T.yb[:, 128:256], T.ps1[:, 0:128], F.Copy))
-    need(ACT, "a", k)
+    na(k)
     ACT.dma_start(T.y[:, 128:256], T.yb[:, 128:256]).then_inc(sem["y1"], 16)
 
     SY.wait_ge(sem["y0"], 16)
     ACT.wait_ge(sem["y1"], 16)
-    g.wait_ge(sem["ls"], sent[0])
+    g.wait_ge(sem["ls"], sent["ls"])
     for name in ("sv", "sa", "st", "sp"):
         g.wait_ge(sem[name], count[name])

@@ -8,11 +8,11 @@ XT = S + RC
 KW = 416
 
 SCRATCH = {}
-for _t, _l in (("int32", "nbi32 li8 ti2 tq2 rli20 cint4 clo4"),
-               ("uint16", "w32 lu8 rl20 fu3 rf16 cp18 pu32"),
-               ("bfloat16", "band1120 mi512 mask512 rs512 junk2048 fx256 fy256 dd256 jf512 jv256 pm1024 pf512 ma512 sba512 "
+for _t, _l in (("int32", "nbi32 nbd32 li8 ti2 tq2 rli20 cint4 clo4"),
+               ("uint16", "w32 wd32 lu8 rl20 rf16 cp18 pu32"),
+               ("bfloat16", "band1120 mi288 mask144 rs288 junk1280 fx256 fy256 dd256 jf512 jv256 pm1024 pf512 pg512 pt512 "
                             "mb288 sbb288 xt1024 at4096 vt1024 ut512 ho1024 hr576"),
-               ("float32", "jd32 thr4 cnt4 cnv4 gh8 gl8 ss4 yb256")):
+               ("float32", "va256 vb256 vc288 jd32 thr4 cnt4 cnv4 gh8 ss4 rq16 yb256")):
     for _e in _l.split():
         _n = _e.rstrip("0123456789")
         SCRATCH[_n] = ("sbuf", [128, int(_e[len(_n):])], _t)
@@ -23,7 +23,7 @@ for _n, _w in (("ca", 1024), ("cv", 256), ("cu", 256), ("x0", S), ("s1", RC), ("
 for _i in range(8):
     SCRATCH["ps%d" % _i] = ("psum", [128, 512], "float32")
 SEMAPHORES = ["sv", "sa", "st", "sp",
-              "ln", "lx", "la0", "la1", "lu_", "lv_", "lb",
+              "ln", "ld", "lw", "lx", "la0", "la1", "la2", "lu_", "lv_",
               "uc", "us", "rq", "xc", "xs", "bc", "bs",
               "lq", "lf", "ls",
               "y0", "y1"]
@@ -139,10 +139,13 @@ def rank_program(g, core, T, topo):
     for r in (0, 16):
         SY.dma_start(T.nbi[r:r + 16, 0:16], T.nb0[:]).then_inc(sem["ln"], 16)
         ACT.dma_start(T.nbi[r:r + 16, 16:32], T.nb1[:]).then_inc(sem["ln"], 16)
+    for r in (0, 1):
+        ACT.dma_start(T.nbd[16 * r:16 * r + 16, 0:16 - r], T.nb0[:, r:16]).then_inc(sem["ld"], 16)
+        ACT.dma_start(T.nbd[16 * r:16 * r + 16, 16:32 - r], T.nb1[:, r:16]).then_inc(sem["ld"], 16)
     SY.dma_start(T.ut[:], T.u[:, 4 * half:4 * half + 512]).then_inc(sem["lu_"], 16)
     SY.dma_start(T.xt[:], T.x[:]).then_inc(sem["lx"], 16)
     SY.dma_start(T.at[:, 0:2048], T.a[:, 0:2048]).then_inc(sem["la0"], 16)
-    SY.dma_start(T.at[:, 2048:4096], T.a[:, 2048:4096]).then_inc(sem["la1"], 16)
+    SY.dma_start(T.at[:, 2048:3072], T.a[:, 2048:3072]).then_inc(sem["la1"], 16)
 
     k_jd = iota(T.jd[:], [[1, 32]], 0, -1)
     iota(T.ti[:], [[0, 2]], 0, 1, whole=True)
@@ -151,7 +154,8 @@ def rank_program(g, core, T, topo):
     iota(T.cnv[:], [[0, 4]])
     k_cn = iota(T.jv[:, 240:256], [[0, 16]], -255)
     iota(T.rli[:], [[16, 2], [32, 10]], whole=True)
-    iota(T.mi[:], [[0, 32], [1, 16]])
+    k_mi = iota(T.mi[:], [[0, 18], [1, 16]])
+    k_own = iota(T.pm[:, S * rank:S * rank + S], [[1, S]], -S)
     k = v(V.memset(T.band[:], 0.0))
     nv(k, k_jd)
     for q in range(n):
@@ -170,34 +174,35 @@ def rank_program(g, core, T, topo):
         k_w = v(V.tensor_copy(T.w[quad(q), :], T.nbi[0:32, :]))
     na(k_w, k_cn)
     for i in range(3):
-        e = 32 if i < 2 else 16
+        e = 32 if i < 2 else 14
         k_ca = a(ACT.activation(T.junk[:, 512 * i:512 * i + 16 * e],
                                 T.band[:, 96 - 32 * i:1120 - 32 * i].indirect(T.w[:, 0:e]),
                                 F.Copy, accum_out=T.cnt[:, i:i + 1]))
     nv(k_w, k_cn)
-    k3 = v(V.tensor_copy(T.junk[:, 1536:2048], T.band[:, 0:1024].indirect(T.w[:, 0:32])))
-    k2 = v(V.tensor_copy(T.junk[:, 1280:1536], T.band[:, 32:1056].indirect(T.w[:, 16:32])))
+    k3 = v(V.tensor_copy(T.va[:], T.band[:, 0:1024].indirect(T.w[:, 0:16])))
     V.wait_ge(sem["lu_"], 16)
     k_u = pack("cu", half, half + 128, T.ut[:])
     nv(k3)
-    v(V.tensor_reduce(T.cnv[:, 3:4], T.junk[:, 1536:2048], X, A.add))
+    k3 = v(V.tensor_tensor(T.vb[:], T.band[:, 0:1024].indirect(T.w[:, 16:32]), T.va[:], A.add))
+    k2 = v(V.tensor_copy(T.vc[:], T.band[:, 32:1056].indirect(T.w[:, 14:32])))
+    nv(k3)
+    v(V.tensor_reduce(T.cnv[:, 3:4], T.vb[:], X, A.add))
     nv(k2)
-    k_cv = v(V.tensor_reduce(T.cnv[:, 2:3], T.junk[:, 1280:1536], X, A.add))
+    k_cv = v(V.tensor_reduce(T.cnv[:, 2:3], T.vc[:], X, A.add))
     need(g, "g", k_u)
     send([(mate, away, codes("cu", half, half + 128), codes("cu", half, half + 128))], "uc")
     send([(mate, lane[mate], scales("cu", half, half + 128), scales("cu", half, half + 128))], "us")
-    k_mi = iota(T.pm[:, S * rank:S * rank + S], [[1, S]], -S)
     nv(k_cv, k_ca)
     k = v(V.tensor_tensor(T.cint[:], T.cnt[:], T.cnv[:], A.add))
     nv(k)
     k_gh = v(V.tensor_scalar(T.gh[:, 0:4], T.cint[:], 1023.5, None, A.is_ge))
     k = v(V.tensor_scalar(T.clo[:], T.cint[:], 1023, None, A.bitwise_and))
-    nv(k)
-    k = v(V.tensor_scalar(T.gl[:, 0:4], T.clo[:], 0.5, None, A.is_ge))
     na(k_gh)
     k_h = a(ACT.activation(T.fx[:, 128:256], T.gh[:, 0:4].indirect(T.lu[:, 0:8]), F.Copy))
     nv(k)
-    k = v(V.tensor_copy(T.fx[:, 0:128], T.gl[:, 0:4].indirect(T.lu[:, 0:8])))
+    k = v(V.tensor_scalar(T.fx[:, 0:128], T.clo[:, 0:4].indirect(T.lu[:, 0:8]), 0.5, None, A.is_ge))
+    na(k_mi)
+    k_rs = a(ACT.activation(T.rs[:], T.mi[:], F.Sign))
     nv(k, k_h)
     k = v(V.transpose(T.fy[:], T.fx[:]))
     nv(k)
@@ -210,25 +215,26 @@ def rank_program(g, core, T, topo):
     k = v(V.tensor_scalar(T.jv[:, 0:255], T.dd[:, 0:255], T.thr[:, 2:3], 2.0, A.is_le, A.mult))
     nv(k)
     k = v(V.tensor_reduce(T.ss[:, 2:3], T.jv[:], X, A.add))
-    nv(k, k_sa)
-    k_fu = v(V.tensor_scalar(T.fu[:], T.ss[:, 0:3], 255.0, 0.5, A.add, A.mult))
 
-    need(g, "g", k_fu)
-    send([(q, lane[q], T.fu[:], T.rf[:, 3 * others(q).index(rank):3 * others(q).index(rank) + 3]) for q in others(rank)], "rq")
+    need(g, "g", k, k_sa)
+    send([(q, lane[q], T.ss[:, 0:3], T.rq[:, 3 * others(q).index(rank):3 * others(q).index(rank) + 3]) for q in others(rank)],
+         "rq")
 
     V.wait_ge(sem["lx"], 16)
-    k_x0 = pack("x0", 0, S, T.xt[:])
-    SY.wait_ge(sem["lq"], sent["lq"])
-    need(SY, "s", k_x0)
-    SY.dma_start(codes("xb", 0, S), codes("x0", 0, S)).then_inc(sem["lb"], 16)
-    SY.dma_start(scales("xb", 0, S), scales("x0", 0, S)).then_inc(sem["lb"], 16)
+    pack("x0", 0, S, T.xt[:])
+    V.wait_ge(sem["ld"], 64)
+    for i in range(2):
+        k_wd = v(V.tensor_copy(T.wd[0:32, i:32:2], T.nbd[0:32, 0:32:2]))
+    need(SY, "s", k_wd)
+    for q in range(1, n):
+        SY.dma_start(T.wd[quad(q), :], T.wd[0:32, :]).then_inc(sem["lw"], 16)
     turn = 0
-    k_pm = [k_mi]
+    k_pm = [k_own]
     for i, q in enumerate(others(rank)):
         base = float(C1 * i - 1)
         for z in range(n):
             out = T.pm[quad(z), S * q:S * q + S]
-            if turn % 2 == 0:
+            if turn % 3 < 2:
                 k_pm.append(v(V.tensor_scalar(out, T.dd[quad(q), :], base, None, A.add)))
             else:
                 k_pm.append(a(ACT.activation(out, T.dd[quad(q), :], F.Copy, bias=base)))
@@ -236,15 +242,13 @@ def rank_program(g, core, T, topo):
     na(*k_pm)
     k_pf = a(ACT.activation(T.pf[:], T.pm[:].indirect(T.w[:, 0:32]), F.Copy))
     nv(k_mi)
-    v(V.tensor_scalar(T.mask[:], T.mi[:], 0.5, T.thr[:, 0:1], A.add, A.is_equal))
-    v(V.tensor_scalar(T.rs[:], T.mi[:], 0.5, None, A.is_ge))
-    v(V.tensor_scalar(T.rl[:], T.rli[:], T.thr[:, 0:1], -0.5, A.add, A.add))
-    V.wait_ge(sem["la0"], 16)
-    k_a0 = pack("ca", 0, 512, T.at[:, 0:2048])
+    k_ma = v(V.tensor_scalar(T.mask[:], T.mi[:, 0:RC], 0.5, T.thr[:, 0:1], A.add, A.is_equal))
+    SY.wait_ge(sem["lq"], sent["lq"])
+    SY.dma_start(T.at[:, 3072:4096], T.a[:, 3072:4096]).then_inc(sem["la2"], 16)
 
     V.wait_ge(sem["rq"], into)
-    for z in others(rank):
-        k_rf = v(V.tensor_copy(T.rf[quad(z), 0:9], T.rf[quad(rank), 0:9]))
+    for z in range(n):
+        k_rf = v(V.tensor_scalar(T.rf[quad(z), 0:9], T.rq[quad(rank), 0:9], 255.0, 0.5, A.add, A.mult))
     nv(k_rf)
     k_c = pick_c("s1", 0, RC, "x0", 0, S, T.rf[:, 0:9])
     na(k_rf)
@@ -256,29 +260,32 @@ def rank_program(g, core, T, topo):
     SY.wait_ge(sem["lf"], sent["lf"])
     SY.dma_start(T.vt[:], T.v[:]).then_inc(sem["lv_"], 16)
 
-    nv(k_c, k_pf, *k_pm)
-    v(V.tensor_tensor(T.ma[:], T.pm[:].indirect(T.w[:, 0:32]), T.mask[:], A.mult))
+    ACT.wait_ge(sem["lw"], 16 * (n - 1))
+    na(k_wd)
+    k_pg = a(ACT.activation(T.pg[:], T.pm[:].indirect(T.wd[:, 0:32]), F.Copy))
+    nv(k_c, k_pf, k_ma, k_rs)
     for i in range(2):
-        k = v(V.tensor_tensor(T.mb[:, RC * i:RC * i + RC], T.pf[:, S * i:S * i + S].indirect(T.rf[:, 0:9]), T.mask[:, 0:RC],
-                              A.mult))
+        k = v(V.tensor_tensor(T.mb[:, RC * i:RC * i + RC], T.pf[:, S * i:S * i + S].indirect(T.rf[:, 0:9]), T.mask[:], A.mult))
     nv(k)
-    k = v(V.tensor_tensor_scan(T.sbb[:], T.rs[:, 0:2 * RC], T.mb[:], 0.0, A.mult, A.add))
-    k_sa = v(V.tensor_tensor_scan(T.sba[:], T.rs[:], T.ma[:], 0.0, A.mult, A.add))
+    k = v(V.tensor_tensor_scan(T.sbb[:], T.rs[:], T.mb[:], 0.0, A.mult, A.add))
     nv(k)
     for i in range(2):
-        v(V.tensor_scalar(T.cp[:, i:18:2], T.sbb[:, RC * i + 15:RC * i + RC:16], float(S), None, A.add))
-    nv(k_sa)
-    k_pu = v(V.tensor_scalar(T.pu[:], T.sba[:, 15:512:16], float(S), None, A.add))
+        k_cp = v(V.tensor_scalar(T.cp[:, i:18:2], T.sbb[:, RC * i + 15:RC * i + RC:16], float(S), None, A.add))
+    k_xb = pack("xb", 0, S, T.xt[:])
+    v(V.tensor_scalar(T.rl[:], T.rli[:], T.thr[:, 0:1], -0.5, A.add, A.add))
+    nv(k_pg)
+    k = v(V.transpose(T.pt[:], T.pg[:]))
+    V.wait_ge(sem["la0"], 16)
+    k_a0 = pack("ca", 0, 512, T.at[:, 0:2048])
+    nv(k)
+    k_pu = v(V.tensor_scalar(T.pu[:], T.pt[:, 0:512:16], float(S), None, A.add))
 
-    V.wait_ge(sem["lb"], 32)
     V.wait_ge(sem["xc"], into)
-    nv(k_pu)
+    nv(k_cp, k_xb)
     pick_c("s2", 0, 160, "xb", 0, XT, T.cp[:, 0:10])
     k_c = pick_c("s2", 160, 2 * RC, "xb", 0, XT, T.cp[:, 10:18])
-    cw0 = pick_c("w2", 0, S, "xb", 0, XT, T.pu[:, 0:16])
-    ACT.wait_ge(sem["lb"], 32)
     ACT.wait_ge(sem["xs"], into)
-    na(k_pu)
+    na(k_cp, k_xb)
     k_s0 = pick_s("s2", 0, 160, "xb", 0, XT, T.cp[:, 0:10])
     V.wait_ge(sem["xs"], into)
     k_s1 = pick_sv("s2", 160, 2 * RC, "xb", 0, XT, T.cp[:, 10:18])
@@ -287,6 +294,9 @@ def rank_program(g, core, T, topo):
     need(g, "g", k_s0, k_s1)
     deal(scales, "s2", "l2", 0, 2 * C1, "bs", "ls")
 
+    nv(k_pu)
+    na(k_pu)
+    cw0 = pick_c("w2", 0, S, "xb", 0, XT, T.pu[:, 0:16])
     cw1 = pick_c("w2", KW, KW + S, "xb", 0, XT, T.pu[:, 16:32])
     sw0 = pick_s("w2", 0, S, "xb", 0, XT, T.pu[:, 0:16])
     sw1 = pick_s("w2", KW, KW + S, "xb", 0, XT, T.pu[:, 16:32])
@@ -303,7 +313,10 @@ def rank_program(g, core, T, topo):
         return a(ACT.activation(out, src, F.Relu, scale=0.05))
 
     V.wait_ge(sem["la1"], 16)
+    V.wait_ge(sem["la2"], 16)
     k_a1 = pack("ca", 512, 1024, T.at[:, 2048:4096])
+    V.wait_ge(sem["lv_"], 16)
+    k_v = pack("cv", 0, S, T.vt[:])
     need(TE, "t", cw0, sw0, k_a0)
     for b in range(4):
         mm(T["ps%d" % b][:, 0:S], "ca", 128 * b, "w2", 0, S, True, False)
@@ -311,42 +324,39 @@ def rank_program(g, core, T, topo):
     ks = [mm(T["ps%d" % b][:, 0:S], "ca", 512 + 128 * b, "w2", KW, S, False, True) for b in range(4)]
     k_ro = []
     for b in range(4):
-        na(ks[b])
-        k_ro.append(relu(b, 0, S, "ho", False))
+        on_v = b == 1
+        need(V if on_v else ACT, "v" if on_v else "a", ks[b])
+        k_ro.append(relu(b, 0, S, "ho", on_v))
 
     V.wait_ge(sem["bc"], into)
-    kc0 = pick_c("w2", S, XT, "l2", 0, 2 * RC, T.rl[:, 0:9])
+    pick_c("w2", S, S + 64, "l2", 0, 2 * RC, T.rl[:, 0:4])
+    kc0 = pick_c("w2", S + 64, XT, "l2", 0, 2 * RC, T.rl[:, 4:9])
     kc1 = pick_c("w2", KW + S, KW + XT, "l2", 0, 2 * RC, T.rl[:, 10:19])
+    ACT.wait_ge(sem["bs"], into)
+    k0 = pick_s("w2", S, S + 64, "l2", 0, 2 * RC, T.rl[:, 0:4])
+    V.wait_ge(sem["bs"], into)
+    k0v = pick_sv("w2", S + 64, XT, "l2", 0, 2 * RC, T.rl[:, 4:9])
+    k1 = pick_s("w2", KW + S, KW + XT, "l2", 0, 2 * RC, T.rl[:, 10:19])
+    need(TE, "t", kc0, k0, k0v)
+    for b in range(4):
+        mm(T["ps%d" % (4 + b)][:, 0:RC], "ca", 128 * b, "w2", S, RC, True, False)
+    need(TE, "t", kc1, k1)
+    ks = [mm(T["ps%d" % (4 + b)][:, 0:RC], "ca", 512 + 128 * b, "w2", KW + S, RC, False, True) for b in range(4)]
     nv(kc0)
     pick_c("xx", 0, S, "w2", 0, XT, T.pu[:, 0:16])
-    V.wait_ge(sem["bs"], into)
-    k1 = pick_sv("w2", KW + S, KW + XT, "l2", 0, 2 * RC, T.rl[:, 10:19])
-    ACT.wait_ge(sem["bs"], into)
-    k0 = pick_s("w2", S, XT, "l2", 0, 2 * RC, T.rl[:, 0:9])
-    need(TE, "t", kc1, k0, k1)
-    ks = []
-    for b in range(4):
-        out = T["ps%d" % (4 + b)][:, 0:RC]
-        mm(out, "ca", 128 * b, "w2", S, RC, True, False)
-        ks.append(mm(out, "ca", 512 + 128 * b, "w2", KW + S, RC, False, True))
-    na(k0)
-    pick_s("xx", 0, S, "w2", 0, XT, T.pu[:, 0:16])
-    V.wait_ge(sem["lv_"], 16)
-    k_v = pack("cv", 0, S, T.vt[:])
     nv(kc1)
     cx1 = pick_c("xx", S, 2 * S, "w2", KW, KW + XT, T.pu[:, 16:32])
-    na(ks[0])
-    kr = [relu(0, 4, RC, "hr", False)]
-    nv(ks[1])
-    kr.append(relu(1, 4, RC, "hr", True))
+    na(k0, k0v)
+    pick_s("xx", 0, S, "w2", 0, XT, T.pu[:, 0:16])
     na(k1)
     sx1 = pick_s("xx", S, 2 * S, "w2", KW, KW + XT, T.pu[:, 16:32])
     nv(*k_ro)
     pack("hb", 0, S, T.ho[:])
-    na(ks[2])
-    kr.append(relu(2, 4, RC, "hr", False))
-    nv(ks[3])
-    kr.append(relu(3, 4, RC, "hr", True))
+    kr = []
+    for b in range(4):
+        on_v = b != 2
+        need(V if on_v else ACT, "v" if on_v else "a", ks[b])
+        kr.append(relu(b, 4, RC, "hr", on_v))
     nv(*kr)
     k_hr = pack("hb", S, XT, T.hr[:])
 
@@ -366,18 +376,17 @@ def rank_program(g, core, T, topo):
             ksc = pick_s("hg", c, c + 128, "hb", 0, XT, T.pu[:, o:o + 8])
             need(TE, "t", kc, ksc)
             ky.append(mm(T["ps%d" % hf][:, 0:128], "cv", 128 * i, "hg", c, 128, False, i == 1))
-            if len(ky) == 3:
-                nv(ky[1])
-                k = v(V.tensor_copy(T.yb[:, 0:128], T.ps0[:, 0:128]))
-                need(SY, "s", k)
-                SY.dma_start(T.y[:, 0:128], T.yb[:, 0:128]).then_inc(sem["y0"], 16)
-    na(ky[3])
-    k = a(ACT.activation(T.yb[:, 128:256], T.ps1[:, 0:128], F.Copy))
+    na(ky[1])
+    k = a(ACT.activation(T.yb[:, 0:128], T.ps0[:, 0:128], F.Copy))
     na(k)
-    ACT.dma_start(T.y[:, 128:256], T.yb[:, 128:256]).then_inc(sem["y1"], 16)
+    ACT.dma_start(T.y[:, 0:128], T.yb[:, 0:128]).then_inc(sem["y0"], 16)
+    nv(ky[3])
+    k = v(V.tensor_copy(T.yb[:, 128:256], T.ps1[:, 0:128]))
+    need(SY, "s", k)
+    SY.dma_start(T.y[:, 128:256], T.yb[:, 128:256]).then_inc(sem["y1"], 16)
 
-    SY.wait_ge(sem["y0"], 16)
-    ACT.wait_ge(sem["y1"], 16)
+    ACT.wait_ge(sem["y0"], 16)
+    SY.wait_ge(sem["y1"], 16)
     g.wait_ge(sem["ls"], sent["ls"])
     for name in ("sv", "sa", "st", "sp"):
         g.wait_ge(sem[name], count[name])

from concourse.bass import DstId, RemoteDMATransfer
from concourse.mybir import dt, AluOpType, AxisListType, ActivationFunctionType

S = 256
C1 = 48
RC = 3 * C1
XT = S + RC
KW = 416

SCRATCH = {}
for _t, _l in (("int32", "nbi32 nbd32 li8 ti2 tq2 rli20 cint4 clo4"),
               ("uint16", "w32 wd32 lu8 rl20 rf16 cp18 pu32"),
               ("bfloat16", "band1120 mi288 mask144 rs288 junk1280 fx256 fy256 dd256 jf512 jv256 pm1024 pf512 pg512 pt512 "
                            "mb288 sbb288 xt1024 at4096 vt1024 ut512 ho1024 hr576"),
               ("float32", "va256 vb256 vc288 jd32 thr4 cnt4 cnv4 gh8 ss4 rq16 yb256")):
    for _e in _l.split():
        _n = _e.rstrip("0123456789")
        SCRATCH[_n] = ("sbuf", [128, int(_e[len(_n):])], _t)
for _n, _w in (("ca", 1024), ("cv", 256), ("cu", 256), ("x0", S), ("s1", RC), ("xb", XT), ("s2", 2 * RC), ("l2", 2 * RC),
               ("w2", KW + XT), ("xx", 2 * S), ("hb", XT), ("hg", 2 * S)):
    SCRATCH[_n + "_c"] = ("sbuf", [128, _w], "float8_e4m3fn_x4")
    SCRATCH[_n + "_s"] = ("sbuf", [128, _w], "uint8")
for _i in range(8):
    SCRATCH["ps%d" % _i] = ("psum", [128, 512], "float32")
SEMAPHORES = ["sv", "sa", "st", "sp",
              "ln", "ld", "lw", "lx", "la0", "la1", "la2", "lu_", "lv_",
              "uc", "us", "rq", "xc", "xs", "bc", "bs",
              "lq", "lf", "ls",
              "y0", "y1"]


def rank_program(g, core, T, topo):
    rank = T.rank_of(core)
    if rank is None:
        return
    A, F, X = AluOpType, ActivationFunctionType, AxisListType.X
    V, ACT, TE, SY = g.vector, g.scalar, g.tensor, g.sync
    sem = T.sem
    cores = list(T.cores)
    n = len(cores)
    count = {"sv": 0, "sa": 0, "st": 0, "sp": 0}
    seen = {}

    def done(name, ins):
        ins.then_inc(sem[name], 1)
        count[name] += 1
        return (name, count[name])

    def v(ins):
        return done("sv", ins)

    def a(ins):
        return done("sa", ins)

    def need(eng, tag, *marks):
        best = {}
        for name, c in marks:
            best[name] = max(best.get(name, 0), c)
        for name, c in best.items():
            if seen.get((tag, name), 0) < c:
                eng.wait_ge(sem[name], c)
                seen[tag, name] = c

    def nv(*marks):
        need(V, "v", *marks)

    def na(*marks):
        need(ACT, "a", *marks)

    def iota(out, pattern, base=0, step=0, whole=False):
        if whole:
            return done("sp", g.iota(out, pattern, base, step))
        return done("sp", g.iota(out, pattern, base, step, allow_small_or_imprecise_dtypes=True))

    def others(r):
        return [q for q in range(n) if q != r]

    def near(r):
        return [q for q in others(r) if topo.chip(cores[q]) == topo.chip(cores[r])]

    def lanes(r):
        me = cores[r]
        off = [q for q in others(r) if q not in near(r)]
        res, used = {}, []
        for i, q in enumerate(off):
            e = topo.engines(me, cores[q])
            k = len(e) // len(off)
            res[q] = e[i * k:(i + 1) * k]
            used += res[q]
        for i, q in enumerate(near(r)):
            e = [x for x in topo.engines(me, cores[q]) if x not in used]
            res[q] = e[i::2 * len(near(r))]
        return res, used

    lane, away = lanes(rank)
    into = sum(len(lanes(q)[0][rank]) for q in others(rank))
    mate = near(rank)[0]
    half = 128 * (rank > mate)
    sent = {"lq": 0, "lf": 0, "ls": 0}

    def send(pieces, rsem, lsem="lq"):
        tr = []
        for q, engines, src, dst in pieces:
            rid, pid, _ = topo.addr(cores[q])
            tr.append(RemoteDMATransfer(dst_ids=[DstId(rid=rid, pnc=pid)], dma_engine_mask=sum(1 << e for e in engines),
                                        remote_sem=sem[rsem], src=src, dst=dst, alu_op=0))
            sent[lsem] += len(engines)
        g.remote_dma_fused(tr, local_sem=sem[lsem])

    def codes(name, lo, hi):
        return T[name + "_c"][:, lo:hi].bitcast(dt.uint8)

    def scales(name, lo, hi):
        return T[name + "_s"][:, lo:hi]

    def deal(kind, src, dst, first, size, rsem, lsem):
        out = []
        for q in others(rank):
            i, j = size * others(rank).index(q), first + size * others(q).index(rank)
            out.append((q, lane[q], kind(src, i, i + size), kind(dst, j, j + size)))
        send(out, rsem, lsem)

    def pick_c(out, lo, hi, win, wlo, whi, off):
        return v(V.tensor_copy(T[out + "_c"][:, lo:hi].bitcast(dt.uint32),
                               T[win + "_c"][:, wlo:whi].bitcast(dt.uint32).indirect(off)))

    def pick_s(out, lo, hi, win, wlo, whi, off):
        return a(ACT.activation(T[out + "_s"][:, lo:hi], T[win + "_s"][:, wlo:whi].indirect(off), F.Copy))

    def pick_sv(out, lo, hi, win, wlo, whi, off):
        return v(V.tensor_copy(T[out + "_s"][:, lo:hi], T[win + "_s"][:, wlo:whi].indirect(off)))

    def pack(name, lo, hi, src):
        return v(V.quantize_mx(T[name + "_c"][:, lo:hi], T[name + "_s"][:, lo:hi], src))

    def quad(q):
        return slice(32 * q, 32 * q + 32)

    for r in (0, 16):
        SY.dma_start(T.nbi[r:r + 16, 0:16], T.nb0[:]).then_inc(sem["ln"], 16)
        ACT.dma_start(T.nbi[r:r + 16, 16:32], T.nb1[:]).then_inc(sem["ln"], 16)
    for r in (0, 1):
        ACT.dma_start(T.nbd[16 * r:16 * r + 16, 0:16 - r], T.nb0[:, r:16]).then_inc(sem["ld"], 16)
        ACT.dma_start(T.nbd[16 * r:16 * r + 16, 16:32 - r], T.nb1[:, r:16]).then_inc(sem["ld"], 16)
    SY.dma_start(T.ut[:], T.u[:, 4 * half:4 * half + 512]).then_inc(sem["lu_"], 16)
    SY.dma_start(T.xt[:], T.x[:]).then_inc(sem["lx"], 16)
    SY.dma_start(T.at[:, 0:2048], T.a[:, 0:2048]).then_inc(sem["la0"], 16)
    SY.dma_start(T.at[:, 2048:3072], T.a[:, 2048:3072]).then_inc(sem["la1"], 16)

    k_jd = iota(T.jd[:], [[1, 32]], 0, -1)
    iota(T.ti[:], [[0, 2]], 0, 1, whole=True)
    k_li = iota(T.li[:], [[1, 4], [0, 2]], whole=True)
    iota(T.cnt[:], [[0, 4]])
    iota(T.cnv[:], [[0, 4]])
    k_cn = iota(T.jv[:, 240:256], [[0, 16]], -255)
    iota(T.rli[:], [[16, 2], [32, 10]], whole=True)
    k_mi = iota(T.mi[:], [[0, 18], [1, 16]])
    k_own = iota(T.pm[:, S * rank:S * rank + S], [[1, S]], -S)
    k = v(V.memset(T.band[:], 0.0))
    nv(k, k_jd)
    for q in range(n):
        c, z = 96 + S * q, float(-32 * q)
        v(V.tensor_scalar(T.band[quad(q), c:c + 32], T.jd[quad(q), :], z, None, A.is_equal))
        v(V.tensor_scalar(T.band[quad(q), c + 128:c + 160], T.jd[quad(q), :], z, 1024.0, A.is_equal, A.mult))
    nv(k_li)
    k = v(V.tensor_scalar(T.tq[:], T.ti[:], 15, None, A.bitwise_and))
    v(V.tensor_copy(T.lu[:], T.li[:]))
    nv(k)
    for c in range(3):
        v(V.tensor_scalar(T.thr[:, c:c + 1], T.tq[:, 0:1], 16 * c + 0.5, None, A.add))

    V.wait_ge(sem["ln"], 64)
    for q in range(n):
        k_w = v(V.tensor_copy(T.w[quad(q), :], T.nbi[0:32, :]))
    na(k_w, k_cn)
    for i in range(3):
        e = 32 if i < 2 else 14
        k_ca = a(ACT.activation(T.junk[:, 512 * i:512 * i + 16 * e],
                                T.band[:, 96 - 32 * i:1120 - 32 * i].indirect(T.w[:, 0:e]),
                                F.Copy, accum_out=T.cnt[:, i:i + 1]))
    nv(k_w, k_cn)
    k3 = v(V.tensor_copy(T.va[:], T.band[:, 0:1024].indirect(T.w[:, 0:16])))
    V.wait_ge(sem["lu_"], 16)
    k_u = pack("cu", half, half + 128, T.ut[:])
    nv(k3)
    k3 = v(V.tensor_tensor(T.vb[:], T.band[:, 0:1024].indirect(T.w[:, 16:32]), T.va[:], A.add))
    k2 = v(V.tensor_copy(T.vc[:], T.band[:, 32:1056].indirect(T.w[:, 14:32])))
    nv(k3)
    v(V.tensor_reduce(T.cnv[:, 3:4], T.vb[:], X, A.add))
    nv(k2)
    k_cv = v(V.tensor_reduce(T.cnv[:, 2:3], T.vc[:], X, A.add))
    need(g, "g", k_u)
    send([(mate, away, codes("cu", half, half + 128), codes("cu", half, half + 128))], "uc")
    send([(mate, lane[mate], scales("cu", half, half + 128), scales("cu", half, half + 128))], "us")
    nv(k_cv, k_ca)
    k = v(V.tensor_tensor(T.cint[:], T.cnt[:], T.cnv[:], A.add))
    nv(k)
    k_gh = v(V.tensor_scalar(T.gh[:, 0:4], T.cint[:], 1023.5, None, A.is_ge))
    k = v(V.tensor_scalar(T.clo[:], T.cint[:], 1023, None, A.bitwise_and))
    na(k_gh)
    k_h = a(ACT.activation(T.fx[:, 128:256], T.gh[:, 0:4].indirect(T.lu[:, 0:8]), F.Copy))
    nv(k)
    k = v(V.tensor_scalar(T.fx[:, 0:128], T.clo[:, 0:4].indirect(T.lu[:, 0:8]), 0.5, None, A.is_ge))
    na(k_mi)
    k_rs = a(ACT.activation(T.rs[:], T.mi[:], F.Sign))
    nv(k, k_h)
    k = v(V.transpose(T.fy[:], T.fx[:]))
    nv(k)
    k_d = v(V.tensor_tensor_scan(T.dd[:], T.fy[:], T.fy[:], 0.0, A.add, A.max))
    na(k_d)
    for c in range(2):
        k_sa = a(ACT.activation(T.jf[:, 256 * c:256 * c + 255], T.dd[:, 0:255], F.Sign, bias=T.thr[:, c:c + 1], scale=-1.0,
                                accum_out=T.ss[:, c:c + 1]))
    nv(k_d)
    k = v(V.tensor_scalar(T.jv[:, 0:255], T.dd[:, 0:255], T.thr[:, 2:3], 2.0, A.is_le, A.mult))
    nv(k)
    k = v(V.tensor_reduce(T.ss[:, 2:3], T.jv[:], X, A.add))

    need(g, "g", k, k_sa)
    send([(q, lane[q], T.ss[:, 0:3], T.rq[:, 3 * others(q).index(rank):3 * others(q).index(rank) + 3]) for q in others(rank)],
         "rq")

    V.wait_ge(sem["lx"], 16)
    pack("x0", 0, S, T.xt[:])
    V.wait_ge(sem["ld"], 64)
    for i in range(2):
        k_wd = v(V.tensor_copy(T.wd[0:32, i:32:2], T.nbd[0:32, 0:32:2]))
    need(SY, "s", k_wd)
    for q in range(1, n):
        SY.dma_start(T.wd[quad(q), :], T.wd[0:32, :]).then_inc(sem["lw"], 16)
    turn = 0
    k_pm = [k_own]
    for i, q in enumerate(others(rank)):
        base = float(C1 * i - 1)
        for z in range(n):
            out = T.pm[quad(z), S * q:S * q + S]
            if turn % 3 < 2:
                k_pm.append(v(V.tensor_scalar(out, T.dd[quad(q), :], base, None, A.add)))
            else:
                k_pm.append(a(ACT.activation(out, T.dd[quad(q), :], F.Copy, bias=base)))
            turn += 1
    na(*k_pm)
    k_pf = a(ACT.activation(T.pf[:], T.pm[:].indirect(T.w[:, 0:32]), F.Copy))
    nv(k_mi)
    k_ma = v(V.tensor_scalar(T.mask[:], T.mi[:, 0:RC], 0.5, T.thr[:, 0:1], A.add, A.is_equal))
    SY.wait_ge(sem["lq"], sent["lq"])
    SY.dma_start(T.at[:, 3072:4096], T.a[:, 3072:4096]).then_inc(sem["la2"], 16)

    V.wait_ge(sem["rq"], into)
    for z in range(n):
        k_rf = v(V.tensor_scalar(T.rf[quad(z), 0:9], T.rq[quad(rank), 0:9], 255.0, 0.5, A.add, A.mult))
    nv(k_rf)
    k_c = pick_c("s1", 0, RC, "x0", 0, S, T.rf[:, 0:9])
    na(k_rf)
    k_s = pick_s("s1", 0, RC, "x0", 0, S, T.rf[:, 0:9])
    need(g, "g", k_c)
    deal(codes, "s1", "xb", S, C1, "xc", "lf")
    need(g, "g", k_s)
    deal(scales, "s1", "xb", S, C1, "xs", "lf")
    SY.wait_ge(sem["lf"], sent["lf"])
    SY.dma_start(T.vt[:], T.v[:]).then_inc(sem["lv_"], 16)

    ACT.wait_ge(sem["lw"], 16 * (n - 1))
    na(k_wd)
    k_pg = a(ACT.activation(T.pg[:], T.pm[:].indirect(T.wd[:, 0:32]), F.Copy))
    nv(k_c, k_pf, k_ma, k_rs)
    for i in range(2):
        k = v(V.tensor_tensor(T.mb[:, RC * i:RC * i + RC], T.pf[:, S * i:S * i + S].indirect(T.rf[:, 0:9]), T.mask[:], A.mult))
    nv(k)
    k = v(V.tensor_tensor_scan(T.sbb[:], T.rs[:], T.mb[:], 0.0, A.mult, A.add))
    nv(k)
    for i in range(2):
        k_cp = v(V.tensor_scalar(T.cp[:, i:18:2], T.sbb[:, RC * i + 15:RC * i + RC:16], float(S), None, A.add))
    k_xb = pack("xb", 0, S, T.xt[:])
    v(V.tensor_scalar(T.rl[:], T.rli[:], T.thr[:, 0:1], -0.5, A.add, A.add))
    nv(k_pg)
    k = v(V.transpose(T.pt[:], T.pg[:]))
    V.wait_ge(sem["la0"], 16)
    k_a0 = pack("ca", 0, 512, T.at[:, 0:2048])
    nv(k)
    k_pu = v(V.tensor_scalar(T.pu[:], T.pt[:, 0:512:16], float(S), None, A.add))

    V.wait_ge(sem["xc"], into)
    nv(k_cp, k_xb)
    pick_c("s2", 0, 160, "xb", 0, XT, T.cp[:, 0:10])
    k_c = pick_c("s2", 160, 2 * RC, "xb", 0, XT, T.cp[:, 10:18])
    ACT.wait_ge(sem["xs"], into)
    na(k_cp, k_xb)
    k_s0 = pick_s("s2", 0, 160, "xb", 0, XT, T.cp[:, 0:10])
    V.wait_ge(sem["xs"], into)
    k_s1 = pick_sv("s2", 160, 2 * RC, "xb", 0, XT, T.cp[:, 10:18])
    need(g, "g", k_c)
    deal(codes, "s2", "l2", 0, 2 * C1, "bc", "ls")
    need(g, "g", k_s0, k_s1)
    deal(scales, "s2", "l2", 0, 2 * C1, "bs", "ls")

    nv(k_pu)
    na(k_pu)
    cw0 = pick_c("w2", 0, S, "xb", 0, XT, T.pu[:, 0:16])
    cw1 = pick_c("w2", KW, KW + S, "xb", 0, XT, T.pu[:, 16:32])
    sw0 = pick_s("w2", 0, S, "xb", 0, XT, T.pu[:, 0:16])
    sw1 = pick_s("w2", KW, KW + S, "xb", 0, XT, T.pu[:, 16:32])

    def mm(out, wt, wcol, mv, c, width, start, stop):
        return done("st", TE.matmul_mx(out, T[wt + "_c"][:, wcol:wcol + 128], T[wt + "_s"][:, wcol:wcol + 128],
                                       T[mv + "_c"][:, c:c + width], T[mv + "_s"][:, c:c + width], start, stop))

    def relu(b, bank, width, tile, on_vector):
        out = T[tile][:, b:4 * width:4]
        src = T["ps%d" % (bank + b)][:, 0:width]
        if on_vector:
            return v(V.tensor_scalar(out, src, 0.0, 0.05, A.max, A.mult))
        return a(ACT.activation(out, src, F.Relu, scale=0.05))

    V.wait_ge(sem["la1"], 16)
    V.wait_ge(sem["la2"], 16)
    k_a1 = pack("ca", 512, 1024, T.at[:, 2048:4096])
    V.wait_ge(sem["lv_"], 16)
    k_v = pack("cv", 0, S, T.vt[:])
    need(TE, "t", cw0, sw0, k_a0)
    for b in range(4):
        mm(T["ps%d" % b][:, 0:S], "ca", 128 * b, "w2", 0, S, True, False)
    need(TE, "t", cw1, sw1, k_a1)
    ks = [mm(T["ps%d" % b][:, 0:S], "ca", 512 + 128 * b, "w2", KW, S, False, True) for b in range(4)]
    k_ro = []
    for b in range(4):
        on_v = b == 1
        need(V if on_v else ACT, "v" if on_v else "a", ks[b])
        k_ro.append(relu(b, 0, S, "ho", on_v))

    V.wait_ge(sem["bc"], into)
    pick_c("w2", S, S + 64, "l2", 0, 2 * RC, T.rl[:, 0:4])
    kc0 = pick_c("w2", S + 64, XT, "l2", 0, 2 * RC, T.rl[:, 4:9])
    kc1 = pick_c("w2", KW + S, KW + XT, "l2", 0, 2 * RC, T.rl[:, 10:19])
    ACT.wait_ge(sem["bs"], into)
    k0 = pick_s("w2", S, S + 64, "l2", 0, 2 * RC, T.rl[:, 0:4])
    V.wait_ge(sem["bs"], into)
    k0v = pick_sv("w2", S + 64, XT, "l2", 0, 2 * RC, T.rl[:, 4:9])
    k1 = pick_s("w2", KW + S, KW + XT, "l2", 0, 2 * RC, T.rl[:, 10:19])
    need(TE, "t", kc0, k0, k0v)
    for b in range(4):
        mm(T["ps%d" % (4 + b)][:, 0:RC], "ca", 128 * b, "w2", S, RC, True, False)
    need(TE, "t", kc1, k1)
    ks = [mm(T["ps%d" % (4 + b)][:, 0:RC], "ca", 512 + 128 * b, "w2", KW + S, RC, False, True) for b in range(4)]
    nv(kc0)
    pick_c("xx", 0, S, "w2", 0, XT, T.pu[:, 0:16])
    nv(kc1)
    cx1 = pick_c("xx", S, 2 * S, "w2", KW, KW + XT, T.pu[:, 16:32])
    na(k0, k0v)
    pick_s("xx", 0, S, "w2", 0, XT, T.pu[:, 0:16])
    na(k1)
    sx1 = pick_s("xx", S, 2 * S, "w2", KW, KW + XT, T.pu[:, 16:32])
    nv(*k_ro)
    pack("hb", 0, S, T.ho[:])
    kr = []
    for b in range(4):
        on_v = b != 2
        need(V if on_v else ACT, "v" if on_v else "a", ks[b])
        kr.append(relu(b, 4, RC, "hr", on_v))
    nv(*kr)
    k_hr = pack("hb", S, XT, T.hr[:])

    TE.wait_ge(sem["uc"], len(lanes(mate)[1]))
    TE.wait_ge(sem["us"], len(lanes(mate)[0][rank]))
    need(TE, "t", cx1, sx1, k_u, k_v, *k_ro)
    for i in range(2):
        for hf in range(2):
            mm(T["ps%d" % hf][:, 0:128], "cu", 128 * i, "xx", S * i + 128 * hf, 128, i == 0, False)
    nv(k_hr)
    na(k_hr)
    ky = []
    for hf in range(2):
        for i in range(2):
            c, o = S * i + 128 * hf, 16 * i + 8 * hf
            kc = pick_c("hg", c, c + 128, "hb", 0, XT, T.pu[:, o:o + 8])
            ksc = pick_s("hg", c, c + 128, "hb", 0, XT, T.pu[:, o:o + 8])
            need(TE, "t", kc, ksc)
            ky.append(mm(T["ps%d" % hf][:, 0:128], "cv", 128 * i, "hg", c, 128, False, i == 1))
    na(ky[1])
    k = a(ACT.activation(T.yb[:, 0:128], T.ps0[:, 0:128], F.Copy))
    na(k)
    ACT.dma_start(T.y[:, 0:128], T.yb[:, 0:128]).then_inc(sem["y0"], 16)
    nv(ky[3])
    k = v(V.tensor_copy(T.yb[:, 128:256], T.ps1[:, 0:128]))
    need(SY, "s", k)
    SY.dma_start(T.y[:, 128:256], T.yb[:, 128:256]).then_inc(sem["y1"], 16)

    ACT.wait_ge(sem["y0"], 16)
    SY.wait_ge(sem["y1"], 16)
    g.wait_ge(sem["ls"], sent["ls"])
    for name in ("sv", "sa", "st", "sp"):
        g.wait_ge(sem[name], count[name])
